import numpy as np
import ml_dtypes


def mxq(x, axis, fmt="e4m3"):
    dtype, down = {"e4m3": (ml_dtypes.float8_e4m3fn, 7), "e5m2": (ml_dtypes.float8_e5m2, 14)}[fmt]
    v = np.moveaxis(np.asarray(x, np.float32).astype(ml_dtypes.bfloat16).astype(np.float64), axis, -1)
    blocks = v.reshape(v.shape[:-1] + (-1, 32))
    amax = np.abs(blocks).max(-1, keepdims=True)
    byte = np.maximum(np.where(amax > 0, np.frexp(amax)[1] - 1 + 127, 0) - down, 1)
    scale = np.exp2(byte - 127.0)
    codes = (blocks / scale).astype(np.float32).astype(dtype).astype(np.float64)
    return np.moveaxis((codes * scale).reshape(v.shape), -1, axis)


WIDE = False


def mx_kscale(k):
    if not WIDE:
        return np.ones(k)
    levels = np.array([10, -10, 5, -5, 0])
    if k % 512:
        return np.exp2(np.random.permutation(np.resize(levels, k // 32))).repeat(32)
    a = np.empty((k // 512, 16))
    for p in range(k // 512):
        a[p, :8] = np.random.permutation(np.resize(levels, 8))
        for g in range(8):
            far = levels[np.abs(levels - a[p, g]) >= 10]
            a[p, g + 8] = far[np.random.randint(len(far))]
    return np.exp2(a.ravel()).repeat(32)


def f64(x):
    return np.asarray(x).astype(np.float64)


def striped(idx):
    return np.tile(idx.reshape(-1, 16).T, (8, 1)).astype(np.uint16)


def unstriped(offs):
    return offs[:16].T.reshape(-1).astype(np.int64)


def pack_weight(w):
    k, n = w.shape
    w = f64(np.asarray(w, np.float32).astype(ml_dtypes.bfloat16)).reshape(k // 32, 32, n)
    amax = np.abs(w).max(1)
    byte = np.clip(np.where(amax > 0, np.frexp(amax)[1] - 1 + 127 - 7, 1), 1, 254)
    scaled = (w * np.exp2(127.0 - byte)[:, None, :]).reshape(k, n).astype(np.float32)
    words = np.ascontiguousarray(scaled.reshape(k // 512, 128, 4, n).transpose(0, 1, 3, 2)).astype(ml_dtypes.float8_e4m3fn).view(np.uint8)
    return words, np.ascontiguousarray(byte.astype(np.uint8).reshape(k // 512, 16, n))


def unpack_weight(words, scales):
    g, p, n, _ = words.shape
    vals = np.ascontiguousarray(words).view(ml_dtypes.float8_e4m3fn).astype(np.float64) * np.repeat(np.exp2(scales.astype(np.float64) - 127.0), 8, axis=1)[..., None]
    return vals.transpose(0, 1, 3, 2).reshape(g * 512, n)


K, T, S, H, D, V, W, U = 512, 1024, 512, 512, 4, 128, 2048, 512


def setup_inputs():
    n = np.random.standard_normal
    s = mx_kscale(K)[:, None]
    u = mx_kscale(H)
    packed_xT = pack_weight(n((K, T)) * s)
    packed_eT = pack_weight(n((H, W)) / np.sqrt(H) / u[:, None])
    return {
        "x_words": packed_xT[0],
        "x_scales": packed_xT[1],
        "w1": (n((K, H)) / np.sqrt(K) / s * u).astype(np.float32),
        "e_words": packed_eT[0],
        "e_scales": packed_eT[1],
        "goal": ((np.random.uniform(size=(S, V)) < 0.01) * 1.0).astype(np.float32),
        "offs": striped(np.random.permutation(T)[:S]),
        "cen": striped(np.random.permutation(W)[:U]),
    }


def reference(x_words, x_scales, w1, e_words, e_scales, goal, offs, cen):
    xq = unpack_weight(x_words, x_scales)[:, unstriped(offs)]
    h = mxq(f64(w1), 0, "e4m3").T @ xq
    e_cen = unpack_weight(e_words, e_scales)[:, unstriped(cen)]
    y = mxq(h, 0, "e4m3").T @ e_cen
    ex = np.exp(2.0 * y)
    es = ex * y
    se = ex.reshape(len(ex), -1, D).sum(axis=2)
    t0 = (es.reshape(len(es), -1, D).sum(axis=2)) / se
    l = 3.0 * (t0 - (0.3 * f64(goal)))
    ex = np.exp(l - l.max(axis=1, keepdims=True))
    return ex / ex.sum(axis=1, keepdims=True) - f64(goal)

@@ -1,0 +1,171 @@
+from contextlib import ExitStack
+
+import concourse.mybir as mybir
+from concourse.masks import make_identity
+
+K, T, S, H, D, V, W, U = 512, 1024, 512, 512, 4, 128, 2048, 512
+FLOPS = 2 * K * H * S + 2 * H * S * U
+
+F32 = mybir.dt.float32
+BF16 = mybir.dt.bfloat16
+I32 = mybir.dt.int32
+U32 = mybir.dt.uint32
+U16 = mybir.dt.uint16
+U8 = mybir.dt.uint8
+FP8X4 = mybir.dt.float8_e4m3fn_x4
+ACT = mybir.ActivationFunctionType
+ALU = mybir.AluOpType
+
+P = 128
+PACK = 4
+BLOCKS = S // P
+HALVES = 2
+
+
+def tile_picked_ystrip_grad_p_kernel(
+    tc, x_words, x_scales, w1, e_words, e_scales, goal, offs, cen, out
+):
+    nc = tc.nc
+    with ExitStack() as ctx:
+        sb = ctx.enter_context(tc.tile_pool(name="sb", bufs=1))
+        ps = ctx.enter_context(tc.psum_pool(name="ps", bufs=1))
+
+        offs_t = sb.tile([P, S // 16], U16, name="offs_t")
+        cen_t = sb.tile([P, U // 16], U16, name="cen_t")
+        xs_win = sb.tile([P, T], U8, name="xs_win", align_bytes=64)
+        es_win = sb.tile([P, W], U8, name="es_win", align_bytes=64)
+        xw_win = sb.tile([P, T], I32, name="xw_win", align_bytes=64)
+        ew_win = sb.tile([P, W], I32, name="ew_win", align_bytes=64)
+        w_raw = [sb.tile([P, PACK, H // HALVES], F32, name="w_raw%d" % i, tag="raw%d" % i, align_bytes=64) for i in range(HALVES)]
+
+        nc.vector.memset(xs_win[:].bitcast(I32), 0)
+        nc.vector.memset(es_win[:].bitcast(I32), 0)
+
+        w_rows = w1.rearrange("(p j) c -> p j c", j=PACK)
+        nc.sync.dma_start(offs_t[:], offs)
+        nc.sync.dma_start(cen_t[:], cen)
+        nc.sync.dma_start(xw_win[:], x_words[0].rearrange("p c r -> p (c r)").bitcast(I32))
+        for i in range(HALVES):
+            nc.sync.dma_start(w_raw[i][:], w_rows[:, :, i * H // HALVES : (i + 1) * H // HALVES])
+        nc.sync.dma_start(ew_win[:], e_words[0].rearrange("p c r -> p (c r)").bitcast(I32))
+        for q in range(4):
+            nc.scalar.dma_start(
+                xs_win[32 * q : 32 * q + 4, :].bitcast(I32), x_scales[0, 4 * q : 4 * q + 4, :].bitcast(I32)
+            )
+        for q in range(4):
+            nc.gpsimd.dma_start(
+                es_win[32 * q : 32 * q + 4, :].bitcast(I32), e_scales[0, 4 * q : 4 * q + 4, :].bitcast(I32)
+            )
+
+        ident = sb.tile([P, P], F32, name="ident")
+        make_identity(nc, ident[:])
+
+        w_bf = sb.tile([P, PACK * H], BF16, name="w_bf", align_bytes=64)
+        w_bf_v = w_bf[:].rearrange("p (t m j) -> p m j t", t=PACK, j=PACK)
+        m_half = P // HALVES
+        for i in range(HALVES):
+            nc.scalar.copy(
+                w_bf_v[:, i * m_half : (i + 1) * m_half],
+                w_raw[i][:].rearrange("p j (m t) -> p m j t", t=PACK),
+            )
+
+        goal_t = sb.tile([P, BLOCKS, V], F32, name="goal_t", tag="raw0", align_bytes=64)
+        nc.sync.dma_start(goal_t[:], goal.rearrange("(b p) v -> p b v", p=P))
+
+        xs_g = sb.tile([P, S], U8, name="xs_g", align_bytes=64)
+        es_g = sb.tile([P, U], U8, name="es_g", align_bytes=64)
+        ew_g = sb.tile([P, U], U32, name="ew_g", align_bytes=64)
+        es_p = sb.tile([P, U], U8, name="es_p", align_bytes=64)
+        ew_p = sb.tile([P, U], U32, name="ew_p", align_bytes=64)
+        xw_g = sb.tile([P, S], U32, name="xw_g", align_bytes=64)
+        w_codes = sb.tile([P, H], U32, name="w_codes", align_bytes=64)
+        w_scales = sb.tile([P, H], U8, name="w_scales", align_bytes=64)
+
+        nc.vector.tensor_copy(xw_g[:], xw_win[:].bitcast(U32).indirect(offs_t[:]))
+        nc.vector.tensor_copy(xs_g[:], xs_win[:].indirect(offs_t[:]))
+        nc.vector.tensor_copy(es_g[:], es_win[:].indirect(cen_t[:]))
+        nc.vector.quantize_mx(out=w_codes[:].bitcast(FP8X4), scales=w_scales[:], in_=w_bf[:])
+        nc.vector.tensor_copy(es_p[:].rearrange("p (d v) -> p v d", d=D), es_g[:].rearrange("p (v d) -> p v d", d=D))
+        nc.vector.tensor_copy(ew_g[:], ew_win[:].bitcast(U32).indirect(cen_t[:]))
+        nc.vector.tensor_copy(ew_p[:].rearrange("p (d v) -> p v d", d=D), ew_g[:].rearrange("p (v d) -> p v d", d=D))
+
+        h_bf = []
+        for b in range(BLOCKS):
+            h_ps = ps.tile([P, PACK, P], F32, name="h_ps%d" % b, tag="bank_a%d" % b)
+            for t in range(PACK):
+                nc.tensor.matmul_mx(
+                    out=h_ps[:, t, :],
+                    lhsT=w_codes[:, t * P : (t + 1) * P].bitcast(FP8X4),
+                    lhsT_scale=w_scales[:, t * P : (t + 1) * P],
+                    rhs=xw_g[:, b * P : (b + 1) * P].bitcast(FP8X4),
+                    rhs_scale=xs_g[:, b * P : (b + 1) * P],
+                    start=True,
+                    stop=True,
+                )
+            hb = sb.tile([P, P, PACK], BF16, name="h_bf%d" % b, align_bytes=64)
+            nc.scalar.copy(hb[:], h_ps[:].rearrange("p t n -> p n t"))
+            h_bf.append(hb)
+
+        se_ps = [ps.tile([P, 2, V], F32, name="se_ps%d" % i, tag="bank_a%d" % i) for i in range(HALVES)]
+        ses_ps = [ps.tile([P, 2, V], F32, name="ses_ps%d" % i, tag="bank_a%d" % (2 + i)) for i in range(HALVES)]
+        for b in range(BLOCKS):
+            half, part = divmod(b, BLOCKS // HALVES)
+            h_codes = sb.tile([P, P], U32, name="h_codes%d" % b, align_bytes=64)
+            h_scales = sb.tile([P, P], U8, name="h_scales%d" % b, align_bytes=64)
+            nc.vector.quantize_mx(
+                out=h_codes[:].bitcast(FP8X4), scales=h_scales[:], in_=h_bf[b][:].rearrange("p n t -> p (n t)")
+            )
+            y_ps = ps.tile([P, D, P], F32, name="y_ps%d" % b, tag="bank_y%d" % b)
+            for d in range(D):
+                nc.tensor.matmul_mx(
+                    out=y_ps[:, d, :],
+                    lhsT=ew_p[:, d * V : (d + 1) * V].bitcast(FP8X4),
+                    lhsT_scale=es_p[:, d * V : (d + 1) * V],
+                    rhs=h_codes[:].bitcast(FP8X4),
+                    rhs_scale=h_scales[:],
+                    start=True,
+                    stop=True,
+                )
+            ex = sb.tile([P, D, P], F32, name="ex%d" % b, align_bytes=64)
+            exy = sb.tile([P, D, P], F32, name="exy%d" % b, align_bytes=64)
+            nc.scalar.activation(ex[:], y_ps[:], ACT.Exp, scale=2.0)
+            nc.vector.tensor_tensor(exy[:], y_ps[:], ex[:], ALU.mult)
+            for src, dst in ((ex, se_ps), (exy, ses_ps)):
+                for d in range(D):
+                    nc.tensor.matmul(
+                        dst[half][:, part, :], src[:, d, :], ident[:],
+                        start=(d == 0), stop=(d == D - 1), is_transpose=True,
+                    )
+
+        root = sb.tile([P, BLOCKS, V], F32, name="root", align_bytes=64)
+        gse = sb.tile([P, BLOCKS, V], F32, name="gse", align_bytes=64)
+        num = sb.tile([P, BLOCKS, V], F32, name="num", align_bytes=64)
+        mid = sb.tile([P, BLOCKS, V], F32, name="mid", align_bytes=64)
+        logit = sb.tile([P, BLOCKS, V], F32, name="logit", align_bytes=64)
+        negmax = [sb.tile([P, 2], F32, name="negmax%d" % i) for i in range(HALVES)]
+        hs = [slice(2 * i, 2 * i + 2) for i in range(HALVES)]
+        for i in range(HALVES):
+            nc.vector.scalar_tensor_tensor(gse[:, hs[i], :], goal_t[:, hs[i], :], -0.9, se_ps[i][:], ALU.mult, ALU.mult)
+        for i in range(HALVES):
+            nc.vector.scalar_tensor_tensor(num[:, hs[i], :], ses_ps[i][:], 3.0, gse[:, hs[i], :], ALU.mult, ALU.add)
+        for i in range(HALVES):
+            nc.scalar.activation(root[:, hs[i], :], se_ps[i][:], ACT.Abs_reciprocal_sqrt)
+        for i in range(HALVES):
+            nc.vector.tensor_tensor(mid[:, hs[i], :], num[:, hs[i], :], root[:, hs[i], :], ALU.mult)
+        for i in range(HALVES):
+            nc.vector.tensor_tensor(logit[:, hs[i], :], mid[:, hs[i], :], root[:, hs[i], :], ALU.mult)
+        for i in range(HALVES):
+            nc.vector.tensor_reduce(negmax[i][:], logit[:, hs[i], :], mybir.AxisListType.X, ALU.max, negate=True)
+
+        for b in range(BLOCKS):
+            half, part = divmod(b, BLOCKS // HALVES)
+            prob = sb.tile([P, V], F32, name="prob%d" % b, align_bytes=64)
+            total = sb.tile([P, 1], F32, name="total%d" % b)
+            inv = sb.tile([P, 1], F32, name="inv%d" % b)
+            res = sb.tile([P, V], F32, name="res%d" % b, align_bytes=64)
+            nc.scalar.activation(
+                prob[:], logit[:, b, :], ACT.Exp, bias=negmax[half][:, part : part + 1], accum_out=total[:]
+            )
+            nc.vector.reciprocal(inv[:], total[:])
+            nc.vector.scalar_tensor_tensor(res[:], prob[:], inv[:], goal_t[:, b, :], ALU.mult, ALU.subtract)
+            nc.sync.dma_start(out[b * P : (b + 1) * P, :], res[:])

@@ -33,29 +33,32 @@ def tile_picked_ystrip_grad_p_kernel(
         offs_t = sb.tile([P, S // 16], U16, name="offs_t")
         cen_t = sb.tile([P, U // 16], U16, name="cen_t")
         xs_win = sb.tile([P, T], U8, name="xs_win", align_bytes=64)
-        es_win = sb.tile([P, W], U8, name="es_win", align_bytes=64)
+        es_win = sb.tile([P, W], U8, name="es_win", tag="es_win", align_bytes=64)
         xw_win = sb.tile([P, T], I32, name="xw_win", align_bytes=64)
-        ew_win = sb.tile([P, W], I32, name="ew_win", align_bytes=64)
-        w_raw = [sb.tile([P, PACK, H // HALVES], F32, name="w_raw%d" % i, tag="raw%d" % i, align_bytes=64) for i in range(HALVES)]
+        ew_win = sb.tile([P, W], I32, name="ew_win", tag="ew_win", align_bytes=64)
+        w_raw = [sb.tile([P, PACK, H // HALVES], F32, name="w_raw%d" % i, align_bytes=64) for i in range(HALVES)]
+
+        goal_t = sb.tile([P, BLOCKS, V], F32, name="goal_t", align_bytes=64)
 
         nc.vector.memset(xs_win[:].bitcast(I32), 0)
         nc.vector.memset(es_win[:].bitcast(I32), 0)
 
         w_rows = w1.rearrange("(p j) c -> p j c", j=PACK)
         nc.sync.dma_start(offs_t[:], offs)
-        nc.sync.dma_start(cen_t[:], cen)
         nc.sync.dma_start(xw_win[:], x_words[0].rearrange("p c r -> p (c r)").bitcast(I32))
-        for i in range(HALVES):
-            nc.sync.dma_start(w_raw[i][:], w_rows[:, :, i * H // HALVES : (i + 1) * H // HALVES])
-        nc.sync.dma_start(ew_win[:], e_words[0].rearrange("p c r -> p (c r)").bitcast(I32))
+        nc.sync.dma_start(cen_t[:], cen)
         for q in range(4):
-            nc.scalar.dma_start(
+            nc.sync.dma_start(
                 xs_win[32 * q : 32 * q + 4, :].bitcast(I32), x_scales[0, 4 * q : 4 * q + 4, :].bitcast(I32)
             )
+        for i in range(HALVES):
+            nc.sync.dma_start(w_raw[i][:], w_rows[:, :, i * H // HALVES : (i + 1) * H // HALVES])
         for q in range(4):
-            nc.gpsimd.dma_start(
+            nc.sync.dma_start(
                 es_win[32 * q : 32 * q + 4, :].bitcast(I32), e_scales[0, 4 * q : 4 * q + 4, :].bitcast(I32)
             )
+        nc.sync.dma_start(ew_win[:], e_words[0].rearrange("p c r -> p (c r)").bitcast(I32))
+        nc.sync.dma_start(goal_t[:], goal.rearrange("(b p) v -> p b v", p=P))
 
         ident = sb.tile([P, P], F32, name="ident")
         make_identity(nc, ident[:])
@@ -69,16 +72,12 @@ def tile_picked_ystrip_grad_p_kernel(
                 w_raw[i][:].rearrange("p j (m t) -> p m j t", t=PACK),
             )
 
-        goal_t = sb.tile([P, BLOCKS, V], F32, name="goal_t", tag="raw0", align_bytes=64)
-        nc.sync.dma_start(goal_t[:], goal.rearrange("(b p) v -> p b v", p=P))
-
         xs_g = sb.tile([P, S], U8, name="xs_g", align_bytes=64)
         es_g = sb.tile([P, U], U8, name="es_g", align_bytes=64)
-        ew_g = sb.tile([P, U], U32, name="ew_g", align_bytes=64)
         es_p = sb.tile([P, U], U8, name="es_p", align_bytes=64)
         ew_p = sb.tile([P, U], U32, name="ew_p", align_bytes=64)
         xw_g = sb.tile([P, S], U32, name="xw_g", align_bytes=64)
-        w_codes = sb.tile([P, H], U32, name="w_codes", align_bytes=64)
+        w_codes = sb.tile([P, H], U32, name="w_codes", tag="es_win", align_bytes=64)
         w_scales = sb.tile([P, H], U8, name="w_scales", align_bytes=64)
 
         nc.vector.tensor_copy(xw_g[:], xw_win[:].bitcast(U32).indirect(offs_t[:]))
@@ -86,15 +85,14 @@ def tile_picked_ystrip_grad_p_kernel(
         nc.vector.tensor_copy(es_g[:], es_win[:].indirect(cen_t[:]))
         nc.vector.quantize_mx(out=w_codes[:].bitcast(FP8X4), scales=w_scales[:], in_=w_bf[:])
         nc.vector.tensor_copy(es_p[:].rearrange("p (d v) -> p v d", d=D), es_g[:].rearrange("p (v d) -> p v d", d=D))
-        nc.vector.tensor_copy(ew_g[:], ew_win[:].bitcast(U32).indirect(cen_t[:]))
-        nc.vector.tensor_copy(ew_p[:].rearrange("p (d v) -> p v d", d=D), ew_g[:].rearrange("p (v d) -> p v d", d=D))
+        nc.vector.tensor_copy(ew_p[:].rearrange("p (d v) -> p v d", d=D), ew_win[:].bitcast(U32).indirect(cen_t[:]))
 
-        h_bf = []
+        h_ps = [ps.tile([P, PACK, P], F32, name="h_ps%d" % b, tag="bank_a%d" % b) for b in range(BLOCKS)]
+        h_bf = [sb.tile([P, P, PACK], BF16, name="h_bf%d" % b, tag="h_bf%d" % (b % (BLOCKS - 1)), align_bytes=64) for b in range(BLOCKS)]
         for b in range(BLOCKS):
-            h_ps = ps.tile([P, PACK, P], F32, name="h_ps%d" % b, tag="bank_a%d" % b)
             for t in range(PACK):
                 nc.tensor.matmul_mx(
-                    out=h_ps[:, t, :],
+                    out=h_ps[b][:, t, :],
                     lhsT=w_codes[:, t * P : (t + 1) * P].bitcast(FP8X4),
                     lhsT_scale=w_scales[:, t * P : (t + 1) * P],
                     rhs=xw_g[:, b * P : (b + 1) * P].bitcast(FP8X4),
@@ -102,39 +100,54 @@ def tile_picked_ystrip_grad_p_kernel(
                     start=True,
                     stop=True,
                 )
-            hb = sb.tile([P, P, PACK], BF16, name="h_bf%d" % b, align_bytes=64)
-            nc.scalar.copy(hb[:], h_ps[:].rearrange("p t n -> p n t"))
-            h_bf.append(hb)
+        for b in range(BLOCKS - 1):
+            nc.scalar.copy(h_bf[b][:], h_ps[b][:].rearrange("p t n -> p n t"))
 
-        se_ps = [ps.tile([P, 2, V], F32, name="se_ps%d" % i, tag="bank_a%d" % i) for i in range(HALVES)]
-        ses_ps = [ps.tile([P, 2, V], F32, name="ses_ps%d" % i, tag="bank_a%d" % (2 + i)) for i in range(HALVES)]
+        h_codes = sb.tile([P, S], U32, name="h_codes", tag="ew_win", align_bytes=64)
+        h_scales = sb.tile([P, S], U8, name="h_scales", align_bytes=64)
+        y_ps = [ps.tile([P, D, P], F32, name="y_ps%d" % b, tag="bank_y%d" % b) for b in range(BLOCKS)]
         for b in range(BLOCKS):
-            half, part = divmod(b, BLOCKS // HALVES)
-            h_codes = sb.tile([P, P], U32, name="h_codes%d" % b, align_bytes=64)
-            h_scales = sb.tile([P, P], U8, name="h_scales%d" % b, align_bytes=64)
+            cols = slice(b * P, (b + 1) * P)
+            if b == BLOCKS // 2:
+                nc.vector.tensor_copy(h_bf[-1][:], h_ps[-1][:].rearrange("p t n -> p n t"))
             nc.vector.quantize_mx(
-                out=h_codes[:].bitcast(FP8X4), scales=h_scales[:], in_=h_bf[b][:].rearrange("p n t -> p (n t)")
+                out=h_codes[:, cols].bitcast(FP8X4),
+                scales=h_scales[:, cols],
+                in_=h_bf[b][:].rearrange("p n t -> p (n t)"),
             )
-            y_ps = ps.tile([P, D, P], F32, name="y_ps%d" % b, tag="bank_y%d" % b)
             for d in range(D):
                 nc.tensor.matmul_mx(
-                    out=y_ps[:, d, :],
+                    out=y_ps[b][:, d, :],
                     lhsT=ew_p[:, d * V : (d + 1) * V].bitcast(FP8X4),
                     lhsT_scale=es_p[:, d * V : (d + 1) * V],
-                    rhs=h_codes[:].bitcast(FP8X4),
-                    rhs_scale=h_scales[:],
+                    rhs=h_codes[:, cols].bitcast(FP8X4),
+                    rhs_scale=h_scales[:, cols],
                     start=True,
                     stop=True,
                 )
-            ex = sb.tile([P, D, P], F32, name="ex%d" % b, align_bytes=64)
-            exy = sb.tile([P, D, P], F32, name="exy%d" % b, align_bytes=64)
-            nc.scalar.activation(ex[:], y_ps[:], ACT.Exp, scale=2.0)
-            nc.vector.tensor_tensor(exy[:], y_ps[:], ex[:], ALU.mult)
-            for src, dst in ((ex, se_ps), (exy, ses_ps)):
-                for d in range(D):
+
+        ex = [sb.tile([P, D, P], F32, name="ex%d" % b, align_bytes=64) for b in range(BLOCKS)]
+        exy = [sb.tile([P, D, P], F32, name="exy%d" % b, align_bytes=64) for b in range(BLOCKS)]
+        for b in range(BLOCKS):
+            nc.scalar.activation(ex[b][:], y_ps[b][:], ACT.Exp, scale=2.0)
+            nc.vector.tensor_tensor(exy[b][:], y_ps[b][:], ex[b][:], ALU.mult)
+
+        se_ps = [ps.tile([P, 2, V], F32, name="se_ps%d" % i, tag="bank_a%d" % i) for i in range(HALVES)]
+        ses_ps = [ps.tile([P, 2, V], F32, name="ses_ps%d" % i, tag="bank_a%d" % (2 + i)) for i in range(HALVES)]
+        addends = []
+        for b in range(BLOCKS - 1):
+            pair = sb.tile([P, D // 2, P], F32, name="pair%d" % b, align_bytes=64)
+            nc.gpsimd.tensor_tensor(pair[:], exy[b][:, : D // 2, :], exy[b][:, D // 2 :, :], ALU.add)
+            addends.append(pair)
+        addends.append(exy[-1])
+        for src, dst in ((ex, se_ps), (addends, ses_ps)):
+            for b in range(BLOCKS):
+                half, part = divmod(b, BLOCKS // HALVES)
+                count = src[b].shape[1]
+                for d in range(count):
                     nc.tensor.matmul(
-                        dst[half][:, part, :], src[:, d, :], ident[:],
-                        start=(d == 0), stop=(d == D - 1), is_transpose=True,
+                        dst[half][:, part, :], src[b][:, d, :], ident[:],
+                        start=(d == 0), stop=(d == count - 1), is_transpose=True,
                     )
 
         root = sb.tile([P, BLOCKS, V], F32, name="root", align_bytes=64)
@@ -146,16 +159,17 @@ def tile_picked_ystrip_grad_p_kernel(
         hs = [slice(2 * i, 2 * i + 2) for i in range(HALVES)]
         for i in range(HALVES):
             nc.vector.scalar_tensor_tensor(gse[:, hs[i], :], goal_t[:, hs[i], :], -0.9, se_ps[i][:], ALU.mult, ALU.mult)
-        for i in range(HALVES):
-            nc.vector.scalar_tensor_tensor(num[:, hs[i], :], ses_ps[i][:], 3.0, gse[:, hs[i], :], ALU.mult, ALU.add)
-        for i in range(HALVES):
             nc.scalar.activation(root[:, hs[i], :], se_ps[i][:], ACT.Abs_reciprocal_sqrt)
-        for i in range(HALVES):
-            nc.vector.tensor_tensor(mid[:, hs[i], :], num[:, hs[i], :], root[:, hs[i], :], ALU.mult)
-        for i in range(HALVES):
-            nc.vector.tensor_tensor(logit[:, hs[i], :], mid[:, hs[i], :], root[:, hs[i], :], ALU.mult)
-        for i in range(HALVES):
-            nc.vector.tensor_reduce(negmax[i][:], logit[:, hs[i], :], mybir.AxisListType.X, ALU.max, negate=True)
+        steps = [
+            lambda i: nc.vector.scalar_tensor_tensor(num[:, hs[i], :], ses_ps[i][:], 3.0, gse[:, hs[i], :], ALU.mult, ALU.add),
+            lambda i: nc.vector.tensor_tensor(mid[:, hs[i], :], num[:, hs[i], :], root[:, hs[i], :], ALU.mult),
+            lambda i: nc.vector.tensor_tensor(logit[:, hs[i], :], mid[:, hs[i], :], root[:, hs[i], :], ALU.mult),
+            lambda i: nc.vector.tensor_reduce(negmax[i][:], logit[:, hs[i], :], mybir.AxisListType.X, ALU.max, negate=True),
+        ]
+        for turn in range(len(steps) + 1):
+            for i in range(HALVES):
+                if 0 <= turn - i < len(steps):
+                    steps[turn - i](i)
 
         for b in range(BLOCKS):
             half, part = divmod(b, BLOCKS // HALVES)

@@ -33,15 +33,15 @@ def tile_picked_ystrip_grad_p_kernel(
         offs_t = sb.tile([P, S // 16], U16, name="offs_t")
         cen_t = sb.tile([P, U // 16], U16, name="cen_t")
         xs_win = sb.tile([P, T], U8, name="xs_win", align_bytes=64)
-        es_win = sb.tile([P, W], U8, name="es_win", tag="es_win", align_bytes=64)
+        es_win = sb.tile([P, W], U8, name="es_win", align_bytes=64)
         xw_win = sb.tile([P, T], I32, name="xw_win", align_bytes=64)
         ew_win = sb.tile([P, W], I32, name="ew_win", tag="ew_win", align_bytes=64)
         w_raw = [sb.tile([P, PACK, H // HALVES], F32, name="w_raw%d" % i, align_bytes=64) for i in range(HALVES)]
 
         goal_t = sb.tile([P, BLOCKS, V], F32, name="goal_t", align_bytes=64)
 
-        nc.vector.memset(xs_win[:].bitcast(I32), 0)
         nc.vector.memset(es_win[:].bitcast(I32), 0)
+        nc.vector.memset(xs_win[:].bitcast(I32), 0)
 
         w_rows = w1.rearrange("(p j) c -> p j c", j=PACK)
         nc.sync.dma_start(offs_t[:], offs)
@@ -49,13 +49,13 @@ def tile_picked_ystrip_grad_p_kernel(
         nc.sync.dma_start(cen_t[:], cen)
         for q in range(4):
             nc.sync.dma_start(
-                xs_win[32 * q : 32 * q + 4, :].bitcast(I32), x_scales[0, 4 * q : 4 * q + 4, :].bitcast(I32)
+                es_win[32 * q : 32 * q + 4, :].bitcast(I32), e_scales[0, 4 * q : 4 * q + 4, :].bitcast(I32)
             )
         for i in range(HALVES):
             nc.sync.dma_start(w_raw[i][:], w_rows[:, :, i * H // HALVES : (i + 1) * H // HALVES])
         for q in range(4):
             nc.sync.dma_start(
-                es_win[32 * q : 32 * q + 4, :].bitcast(I32), e_scales[0, 4 * q : 4 * q + 4, :].bitcast(I32)
+                xs_win[32 * q : 32 * q + 4, :].bitcast(I32), x_scales[0, 4 * q : 4 * q + 4, :].bitcast(I32)
             )
         nc.sync.dma_start(ew_win[:], e_words[0].rearrange("p c r -> p (c r)").bitcast(I32))
         nc.sync.dma_start(goal_t[:], goal.rearrange("(b p) v -> p b v", p=P))
@@ -63,7 +63,7 @@ def tile_picked_ystrip_grad_p_kernel(
         ident = sb.tile([P, P], F32, name="ident")
         make_identity(nc, ident[:])
 
-        w_bf = sb.tile([P, PACK * H], BF16, name="w_bf", align_bytes=64)
+        w_bf = sb.tile([P, PACK * H], BF16, name="w_bf", tag="w_bf", align_bytes=64)
         w_bf_v = w_bf[:].rearrange("p (t m j) -> p m j t", t=PACK, j=PACK)
         m_half = P // HALVES
         for i in range(HALVES):
@@ -72,19 +72,23 @@ def tile_picked_ystrip_grad_p_kernel(
                 w_raw[i][:].rearrange("p j (m t) -> p m j t", t=PACK),
             )
 
-        xs_g = sb.tile([P, S], U8, name="xs_g", align_bytes=64)
+        half_s = S // HALVES
+        xs_early = sb.tile([P, half_s], U8, name="xs_early", align_bytes=64)
+        xs_late = sb.tile([P, half_s], U8, name="xs_late", tag="w_bf", align_bytes=64)
+        xs_g = [half[:, part * P : (part + 1) * P] for half in (xs_early, xs_late) for part in range(2)]
         es_g = sb.tile([P, U], U8, name="es_g", align_bytes=64)
         es_p = sb.tile([P, U], U8, name="es_p", align_bytes=64)
         ew_p = sb.tile([P, U], U32, name="ew_p", align_bytes=64)
         xw_g = sb.tile([P, S], U32, name="xw_g", align_bytes=64)
-        w_codes = sb.tile([P, H], U32, name="w_codes", tag="es_win", align_bytes=64)
+        w_codes = sb.tile([P, H], U32, name="w_codes", align_bytes=64)
         w_scales = sb.tile([P, H], U8, name="w_scales", align_bytes=64)
 
         nc.vector.tensor_copy(xw_g[:], xw_win[:].bitcast(U32).indirect(offs_t[:]))
-        nc.vector.tensor_copy(xs_g[:], xs_win[:].indirect(offs_t[:]))
         nc.vector.tensor_copy(es_g[:], es_win[:].indirect(cen_t[:]))
+        nc.vector.tensor_copy(es_p[:].rearrange("p (d v) -> p d v", d=D), es_g[:].rearrange("p (v d) -> p d v", d=D))
+        nc.vector.tensor_copy(xs_early[:], xs_win[:].indirect(offs_t[:, : half_s // 16]))
         nc.vector.quantize_mx(out=w_codes[:].bitcast(FP8X4), scales=w_scales[:], in_=w_bf[:])
-        nc.vector.tensor_copy(es_p[:].rearrange("p (d v) -> p v d", d=D), es_g[:].rearrange("p (v d) -> p v d", d=D))
+        nc.vector.tensor_copy(xs_late[:], xs_win[:].indirect(offs_t[:, half_s // 16 :]))
         nc.vector.tensor_copy(ew_p[:].rearrange("p (d v) -> p v d", d=D), ew_win[:].bitcast(U32).indirect(cen_t[:]))
 
         h_ps = [ps.tile([P, PACK, P], F32, name="h_ps%d" % b, tag="bank_a%d" % b) for b in range(BLOCKS)]
@@ -96,7 +100,7 @@ def tile_picked_ystrip_grad_p_kernel(
                     lhsT=w_codes[:, t * P : (t + 1) * P].bitcast(FP8X4),
                     lhsT_scale=w_scales[:, t * P : (t + 1) * P],
                     rhs=xw_g[:, b * P : (b + 1) * P].bitcast(FP8X4),
-                    rhs_scale=xs_g[:, b * P : (b + 1) * P],
+                    rhs_scale=xs_g[b],
                     start=True,
                     stop=True,
                 )
@@ -135,11 +139,11 @@ def tile_picked_ystrip_grad_p_kernel(
         se_ps = [ps.tile([P, 2, V], F32, name="se_ps%d" % i, tag="bank_a%d" % i) for i in range(HALVES)]
         ses_ps = [ps.tile([P, 2, V], F32, name="ses_ps%d" % i, tag="bank_a%d" % (2 + i)) for i in range(HALVES)]
         addends = []
-        for b in range(BLOCKS - 1):
+        for b in range(BLOCKS // 2):
             pair = sb.tile([P, D // 2, P], F32, name="pair%d" % b, align_bytes=64)
             nc.gpsimd.tensor_tensor(pair[:], exy[b][:, : D // 2, :], exy[b][:, D // 2 :, :], ALU.add)
             addends.append(pair)
-        addends.append(exy[-1])
+        addends.extend(exy[BLOCKS // 2 :])
         for src, dst in ((ex, se_ps), (addends, ses_ps)):
             for b in range(BLOCKS):
                 half, part = divmod(b, BLOCKS // HALVES)
@@ -166,10 +170,9 @@ def tile_picked_ystrip_grad_p_kernel(
             lambda i: nc.vector.tensor_tensor(logit[:, hs[i], :], mid[:, hs[i], :], root[:, hs[i], :], ALU.mult),
             lambda i: nc.vector.tensor_reduce(negmax[i][:], logit[:, hs[i], :], mybir.AxisListType.X, ALU.max, negate=True),
         ]
-        for turn in range(len(steps) + 1):
+        for step in steps:
             for i in range(HALVES):
-                if 0 <= turn - i < len(steps):
-                    steps[turn - i](i)
+                step(i)
 
         for b in range(BLOCKS):
             half, part = divmod(b, BLOCKS // HALVES)

@@ -47,16 +47,12 @@ def tile_picked_ystrip_grad_p_kernel(
         nc.sync.dma_start(offs_t[:], offs)
         nc.sync.dma_start(xw_win[:], x_words[0].rearrange("p c r -> p (c r)").bitcast(I32))
         nc.sync.dma_start(cen_t[:], cen)
-        for q in range(4):
-            nc.sync.dma_start(
-                es_win[32 * q : 32 * q + 4, :].bitcast(I32), e_scales[0, 4 * q : 4 * q + 4, :].bitcast(I32)
-            )
+        for r in range(4):
+            nc.sync.dma_start(es_win[r:P:32, :].bitcast(I32), e_scales[0, r:16:4, :].bitcast(I32))
         for i in range(HALVES):
             nc.sync.dma_start(w_raw[i][:], w_rows[:, :, i * H // HALVES : (i + 1) * H // HALVES])
-        for q in range(4):
-            nc.sync.dma_start(
-                xs_win[32 * q : 32 * q + 4, :].bitcast(I32), x_scales[0, 4 * q : 4 * q + 4, :].bitcast(I32)
-            )
+        for r in range(4):
+            nc.sync.dma_start(xs_win[r:P:32, :].bitcast(I32), x_scales[0, r:16:4, :].bitcast(I32))
         nc.sync.dma_start(ew_win[:], e_words[0].rearrange("p c r -> p (c r)").bitcast(I32))
         nc.sync.dma_start(goal_t[:], goal.rearrange("(b p) v -> p b v", p=P))
 
@@ -72,10 +68,10 @@ def tile_picked_ystrip_grad_p_kernel(
                 w_raw[i][:].rearrange("p j (m t) -> p m j t", t=PACK),
             )
 
-        half_s = S // HALVES
-        xs_early = sb.tile([P, half_s], U8, name="xs_early", align_bytes=64)
-        xs_late = sb.tile([P, half_s], U8, name="xs_late", tag="w_bf", align_bytes=64)
-        xs_g = [half[:, part * P : (part + 1) * P] for half in (xs_early, xs_late) for part in range(2)]
+        early = S - P
+        xs_early = sb.tile([P, early], U8, name="xs_early", align_bytes=64)
+        xs_late = sb.tile([P, P], U8, name="xs_late", tag="w_bf", align_bytes=64)
+        xs_g = [xs_early[:, b * P : (b + 1) * P] for b in range(BLOCKS - 1)] + [xs_late[:]]
         es_g = sb.tile([P, U], U8, name="es_g", align_bytes=64)
         es_p = sb.tile([P, U], U8, name="es_p", align_bytes=64)
         ew_p = sb.tile([P, U], U32, name="ew_p", align_bytes=64)
@@ -86,9 +82,9 @@ def tile_picked_ystrip_grad_p_kernel(
         nc.vector.tensor_copy(xw_g[:], xw_win[:].bitcast(U32).indirect(offs_t[:]))
         nc.vector.tensor_copy(es_g[:], es_win[:].indirect(cen_t[:]))
         nc.vector.tensor_copy(es_p[:].rearrange("p (d v) -> p d v", d=D), es_g[:].rearrange("p (v d) -> p d v", d=D))
-        nc.vector.tensor_copy(xs_early[:], xs_win[:].indirect(offs_t[:, : half_s // 16]))
+        nc.vector.tensor_copy(xs_early[:], xs_win[:].indirect(offs_t[:, : early // 16]))
         nc.vector.quantize_mx(out=w_codes[:].bitcast(FP8X4), scales=w_scales[:], in_=w_bf[:])
-        nc.vector.tensor_copy(xs_late[:], xs_win[:].indirect(offs_t[:, half_s // 16 :]))
+        nc.vector.tensor_copy(xs_late[:], xs_win[:].indirect(offs_t[:, early // 16 :]))
         nc.vector.tensor_copy(ew_p[:].rearrange("p (d v) -> p v d", d=D), ew_win[:].bitcast(U32).indirect(cen_t[:]))
 
         h_ps = [ps.tile([P, PACK, P], F32, name="h_ps%d" % b, tag="bank_a%d" % b) for b in range(BLOCKS)]

@@ -38,22 +38,22 @@ def tile_picked_ystrip_grad_p_kernel(
         ew_win = sb.tile([P, W], I32, name="ew_win", tag="ew_win", align_bytes=64)
         w_raw = [sb.tile([P, PACK, H // HALVES], F32, name="w_raw%d" % i, align_bytes=64) for i in range(HALVES)]
 
-        goal_t = sb.tile([P, BLOCKS, V], F32, name="goal_t", align_bytes=64)
 
-        nc.vector.memset(es_win[:].bitcast(I32), 0)
-        nc.vector.memset(xs_win[:].bitcast(I32), 0)
+        nc.gpsimd.memset(xs_win[:].bitcast(I32), 0)
+        nc.gpsimd.memset(es_win[:].bitcast(I32), 0)
 
         w_rows = w1.rearrange("(p j) c -> p j c", j=PACK)
         nc.sync.dma_start(offs_t[:], offs)
-        nc.sync.dma_start(xw_win[:], x_words[0].rearrange("p c r -> p (c r)").bitcast(I32))
         nc.sync.dma_start(cen_t[:], cen)
-        for r in range(4):
-            nc.sync.dma_start(es_win[r:P:32, :].bitcast(I32), e_scales[0, r:16:4, :].bitcast(I32))
-        for i in range(HALVES):
-            nc.sync.dma_start(w_raw[i][:], w_rows[:, :, i * H // HALVES : (i + 1) * H // HALVES])
+        nc.sync.dma_start(w_raw[0][:], w_rows[:, :, : H // HALVES])
         for r in range(4):
             nc.sync.dma_start(xs_win[r:P:32, :].bitcast(I32), x_scales[0, r:16:4, :].bitcast(I32))
+        nc.sync.dma_start(w_raw[1][:], w_rows[:, :, H // HALVES :])
+        nc.sync.dma_start(es_win[0:16, :].bitcast(I32), e_scales[0].bitcast(I32))
+        nc.sync.dma_start(xw_win[:], x_words[0].rearrange("p c r -> p (c r)").bitcast(I32))
         nc.sync.dma_start(ew_win[:], e_words[0].rearrange("p c r -> p (c r)").bitcast(I32))
+
+        goal_t = sb.tile([P, BLOCKS, V], F32, name="goal_t", align_bytes=64)
         nc.sync.dma_start(goal_t[:], goal.rearrange("(b p) v -> p b v", p=P))
 
         ident = sb.tile([P, P], F32, name="ident")
@@ -68,10 +68,8 @@ def tile_picked_ystrip_grad_p_kernel(
                 w_raw[i][:].rearrange("p j (m t) -> p m j t", t=PACK),
             )
 
-        early = S - P
-        xs_early = sb.tile([P, early], U8, name="xs_early", align_bytes=64)
-        xs_late = sb.tile([P, P], U8, name="xs_late", tag="w_bf", align_bytes=64)
-        xs_g = [xs_early[:, b * P : (b + 1) * P] for b in range(BLOCKS - 1)] + [xs_late[:]]
+        xs_all = sb.tile([P, S], U8, name="xs_all", align_bytes=64)
+        xs_g = [xs_all[:, b * P : (b + 1) * P] for b in range(BLOCKS)]
         es_g = sb.tile([P, U], U8, name="es_g", align_bytes=64)
         es_p = sb.tile([P, U], U8, name="es_p", align_bytes=64)
         ew_p = sb.tile([P, U], U32, name="ew_p", align_bytes=64)
@@ -79,13 +77,15 @@ def tile_picked_ystrip_grad_p_kernel(
         w_codes = sb.tile([P, H], U32, name="w_codes", align_bytes=64)
         w_scales = sb.tile([P, H], U8, name="w_scales", align_bytes=64)
 
-        nc.vector.tensor_copy(xw_g[:], xw_win[:].bitcast(U32).indirect(offs_t[:]))
+        nc.gpsimd.memset(es_p[:].bitcast(I32), 0)
+        nc.vector.tensor_copy(xs_all[:], xs_win[:].indirect(offs_t[:]))
         nc.vector.tensor_copy(es_g[:], es_win[:].indirect(cen_t[:]))
-        nc.vector.tensor_copy(es_p[:].rearrange("p (d v) -> p d v", d=D), es_g[:].rearrange("p (v d) -> p d v", d=D))
-        nc.vector.tensor_copy(xs_early[:], xs_win[:].indirect(offs_t[:, : early // 16]))
+        for q in range(4):
+            nc.sync.dma_start(es_p[32 * q : 32 * q + 4, :].bitcast(I32), es_g[4 * q : 4 * q + 4, :].bitcast(I32))
         nc.vector.quantize_mx(out=w_codes[:].bitcast(FP8X4), scales=w_scales[:], in_=w_bf[:])
-        nc.vector.tensor_copy(xs_late[:], xs_win[:].indirect(offs_t[:, early // 16 :]))
-        nc.vector.tensor_copy(ew_p[:].rearrange("p (d v) -> p v d", d=D), ew_win[:].bitcast(U32).indirect(cen_t[:]))
+        for lo, hi in ((0, P), (P, 2 * P), (2 * P, S)):
+            nc.vector.tensor_copy(xw_g[:, lo:hi], xw_win[:].bitcast(U32).indirect(offs_t[:, lo // 16 : hi // 16]))
+        nc.vector.tensor_copy(ew_p[:], ew_win[:].bitcast(U32).indirect(cen_t[:]))
 
         h_ps = [ps.tile([P, PACK, P], F32, name="h_ps%d" % b, tag="bank_a%d" % b) for b in range(BLOCKS)]
         h_bf = [sb.tile([P, P, PACK], BF16, name="h_bf%d" % b, tag="h_bf%d" % (b % (BLOCKS - 1)), align_bytes=64) for b in range(BLOCKS)]
@@ -105,7 +105,7 @@ def tile_picked_ystrip_grad_p_kernel(
 
         h_codes = sb.tile([P, S], U32, name="h_codes", tag="ew_win", align_bytes=64)
         h_scales = sb.tile([P, S], U8, name="h_scales", align_bytes=64)
-        y_ps = [ps.tile([P, D, P], F32, name="y_ps%d" % b, tag="bank_y%d" % b) for b in range(BLOCKS)]
+        y_ps = [ps.tile([P, U], F32, name="y_ps%d" % b, tag="bank_y%d" % b) for b in range(BLOCKS)]
         for b in range(BLOCKS):
             cols = slice(b * P, (b + 1) * P)
             if b == BLOCKS // 2:
@@ -115,70 +115,74 @@ def tile_picked_ystrip_grad_p_kernel(
                 scales=h_scales[:, cols],
                 in_=h_bf[b][:].rearrange("p n t -> p (n t)"),
             )
-            for d in range(D):
-                nc.tensor.matmul_mx(
-                    out=y_ps[b][:, d, :],
-                    lhsT=ew_p[:, d * V : (d + 1) * V].bitcast(FP8X4),
-                    lhsT_scale=es_p[:, d * V : (d + 1) * V],
-                    rhs=h_codes[:, cols].bitcast(FP8X4),
-                    rhs_scale=h_scales[:, cols],
-                    start=True,
-                    stop=True,
-                )
+            nc.tensor.matmul_mx(
+                out=y_ps[b][:],
+                lhsT=h_codes[:, cols].bitcast(FP8X4),
+                lhsT_scale=h_scales[:, cols],
+                rhs=ew_p[:].bitcast(FP8X4),
+                rhs_scale=es_p[:],
+                start=True,
+                stop=True,
+            )
 
-        ex = [sb.tile([P, D, P], F32, name="ex%d" % b, align_bytes=64) for b in range(BLOCKS)]
-        exy = [sb.tile([P, D, P], F32, name="exy%d" % b, align_bytes=64) for b in range(BLOCKS)]
+        ex = [sb.tile([P, D, V], F32, name="ex%d" % b, align_bytes=64) for b in range(BLOCKS)]
+        exy = [sb.tile([P, D, V], F32, name="exy%d" % b, align_bytes=64) for b in range(BLOCKS)]
         for b in range(BLOCKS):
-            nc.scalar.activation(ex[b][:], y_ps[b][:], ACT.Exp, scale=2.0)
-            nc.vector.tensor_tensor(exy[b][:], y_ps[b][:], ex[b][:], ALU.mult)
+            y_dv = y_ps[b][:].rearrange("p (v d) -> p d v", d=D)
+            nc.scalar.activation(ex[b][:], y_dv, ACT.Exp, scale=2.0)
+            nc.vector.tensor_tensor(exy[b][:], y_dv, ex[b][:], ALU.mult)
 
-        se_ps = [ps.tile([P, 2, V], F32, name="se_ps%d" % i, tag="bank_a%d" % i) for i in range(HALVES)]
-        ses_ps = [ps.tile([P, 2, V], F32, name="ses_ps%d" % i, tag="bank_a%d" % (2 + i)) for i in range(HALVES)]
-        addends = []
-        for b in range(BLOCKS // 2):
-            pair = sb.tile([P, D // 2, P], F32, name="pair%d" % b, align_bytes=64)
-            nc.gpsimd.tensor_tensor(pair[:], exy[b][:, : D // 2, :], exy[b][:, D // 2 :, :], ALU.add)
-            addends.append(pair)
-        addends.extend(exy[BLOCKS // 2 :])
-        for src, dst in ((ex, se_ps), (addends, ses_ps)):
+        se_ps = ps.tile([P, BLOCKS, P], F32, name="se_ps", tag="bank_a0")
+        ses_ps = ps.tile([P, BLOCKS, P], F32, name="ses_ps", tag="bank_a1")
+        addends = {}
+        for b in range(BLOCKS):
+            for kind, src in (("e", ex), ("y", exy)):
+                addends[kind, b] = src[b]
+                if kind == "y" and b < BLOCKS // 2:
+                    pair = sb.tile([P, D // 2, V], F32, name="pair%s%d" % (kind, b), align_bytes=64)
+                    nc.gpsimd.tensor_tensor(pair[:], src[b][:, : D // 2, :], src[b][:, D // 2 :, :], ALU.add)
+                    addends[kind, b] = pair
+        for kind, dst in (("e", se_ps), ("y", ses_ps)):
             for b in range(BLOCKS):
-                half, part = divmod(b, BLOCKS // HALVES)
-                count = src[b].shape[1]
+                src = addends[kind, b]
+                count = src.shape[1]
                 for d in range(count):
                     nc.tensor.matmul(
-                        dst[half][:, part, :], src[b][:, d, :], ident[:],
+                        dst[:, b, :], src[:, d, :], ident[:],
                         start=(d == 0), stop=(d == count - 1), is_transpose=True,
                     )
 
-        root = sb.tile([P, BLOCKS, V], F32, name="root", align_bytes=64)
-        gse = sb.tile([P, BLOCKS, V], F32, name="gse", align_bytes=64)
-        num = sb.tile([P, BLOCKS, V], F32, name="num", align_bytes=64)
-        mid = sb.tile([P, BLOCKS, V], F32, name="mid", align_bytes=64)
-        logit = sb.tile([P, BLOCKS, V], F32, name="logit", align_bytes=64)
-        negmax = [sb.tile([P, 2], F32, name="negmax%d" % i) for i in range(HALVES)]
+        goal_ps = ps.tile([P, BLOCKS, P], F32, name="goal_ps", tag="bank_y0")
+        for b in range(BLOCKS):
+            nc.tensor.transpose(goal_ps[:, b, :], goal_t[:, b, :], ident[:])
+
+        margin = sb.tile([P, BLOCKS, P], F32, name="margin", align_bytes=64)
+        nc.vector.tensor_scalar(margin[:], goal_ps[:], -0.9, None, ALU.mult)
+        logit_ps = [ps.tile([P, V], F32, name="logit_ps%d" % b, tag=("bank_a2", "bank_a3", "bank_y1", "bank_y2")[b]) for b in range(BLOCKS)]
+        for b in range(BLOCKS):
+            nc.tensor.matmul(logit_ps[b][:], margin[:, b, :], ident[:], start=True, stop=False, is_transpose=True)
+
+        root = sb.tile([P, BLOCKS, P], F32, name="root", align_bytes=64)
+        mid = sb.tile([P, BLOCKS, P], F32, name="mid", align_bytes=64)
+        mean3 = sb.tile([P, BLOCKS, P], F32, name="mean3", align_bytes=64)
+        negmax = [sb.tile([P, 1], F32, name="negmax%d" % b) for b in range(BLOCKS)]
         hs = [slice(2 * i, 2 * i + 2) for i in range(HALVES)]
         for i in range(HALVES):
-            nc.vector.scalar_tensor_tensor(gse[:, hs[i], :], goal_t[:, hs[i], :], -0.9, se_ps[i][:], ALU.mult, ALU.mult)
-            nc.scalar.activation(root[:, hs[i], :], se_ps[i][:], ACT.Abs_reciprocal_sqrt)
-        steps = [
-            lambda i: nc.vector.scalar_tensor_tensor(num[:, hs[i], :], ses_ps[i][:], 3.0, gse[:, hs[i], :], ALU.mult, ALU.add),
-            lambda i: nc.vector.tensor_tensor(mid[:, hs[i], :], num[:, hs[i], :], root[:, hs[i], :], ALU.mult),
-            lambda i: nc.vector.tensor_tensor(logit[:, hs[i], :], mid[:, hs[i], :], root[:, hs[i], :], ALU.mult),
-            lambda i: nc.vector.tensor_reduce(negmax[i][:], logit[:, hs[i], :], mybir.AxisListType.X, ALU.max, negate=True),
-        ]
-        for step in steps:
-            for i in range(HALVES):
-                step(i)
+            nc.scalar.activation(root[:, hs[i], :], se_ps[:, hs[i], :], ACT.Abs_reciprocal_sqrt)
+        for i in range(HALVES):
+            nc.vector.scalar_tensor_tensor(mid[:, hs[i], :], ses_ps[:, hs[i], :], 3.0, root[:, hs[i], :], ALU.mult, ALU.mult)
+        for i in range(HALVES):
+            nc.vector.tensor_tensor(mean3[:, hs[i], :], mid[:, hs[i], :], root[:, hs[i], :], ALU.mult)
+        for b in range(BLOCKS):
+            nc.tensor.matmul(logit_ps[b][:], mean3[:, b, :], ident[:], start=False, stop=True, is_transpose=True)
+            nc.vector.tensor_reduce(negmax[b][:], logit_ps[b][:], mybir.AxisListType.X, ALU.max, negate=True)
 
         for b in range(BLOCKS):
-            half, part = divmod(b, BLOCKS // HALVES)
             prob = sb.tile([P, V], F32, name="prob%d" % b, align_bytes=64)
             total = sb.tile([P, 1], F32, name="total%d" % b)
             inv = sb.tile([P, 1], F32, name="inv%d" % b)
             res = sb.tile([P, V], F32, name="res%d" % b, align_bytes=64)
-            nc.scalar.activation(
-                prob[:], logit[:, b, :], ACT.Exp, bias=negmax[half][:, part : part + 1], accum_out=total[:]
-            )
+            nc.scalar.activation(prob[:], logit_ps[b][:], ACT.Exp, bias=negmax[b][:], accum_out=total[:])
             nc.vector.reciprocal(inv[:], total[:])
             nc.vector.scalar_tensor_tensor(res[:], prob[:], inv[:], goal_t[:, b, :], ALU.mult, ALU.subtract)
             nc.sync.dma_start(out[b * P : (b + 1) * P, :], res[:])

@@ -35,7 +35,7 @@ def tile_picked_ystrip_grad_p_kernel(
         xs_win = sb.tile([P, T], U8, name="xs_win", align_bytes=64)
         es_win = sb.tile([P, W], U8, name="es_win", align_bytes=64)
         xw_win = sb.tile([P, T], I32, name="xw_win", align_bytes=64)
-        ew_win = sb.tile([P, W], I32, name="ew_win", tag="ew_win", align_bytes=64)
+        ew_win = sb.tile([P, W], I32, name="ew_win", align_bytes=64)
         w_raw = [sb.tile([P, PACK, H // HALVES], F32, name="w_raw%d" % i, align_bytes=64) for i in range(HALVES)]
 
 
@@ -70,7 +70,7 @@ def tile_picked_ystrip_grad_p_kernel(
 
         xs_all = sb.tile([P, S], U8, name="xs_all", align_bytes=64)
         xs_g = [xs_all[:, b * P : (b + 1) * P] for b in range(BLOCKS)]
-        es_g = sb.tile([P, U], U8, name="es_g", align_bytes=64)
+        es_g = sb.tile([P, U], U8, name="es_g", tag="es_g", align_bytes=64)
         es_p = sb.tile([P, U], U8, name="es_p", align_bytes=64)
         ew_p = sb.tile([P, U], U32, name="ew_p", align_bytes=64)
         xw_g = sb.tile([P, S], U32, name="xw_g", align_bytes=64)
@@ -82,13 +82,14 @@ def tile_picked_ystrip_grad_p_kernel(
         nc.vector.tensor_copy(es_g[:], es_win[:].indirect(cen_t[:]))
         for q in range(4):
             nc.sync.dma_start(es_p[32 * q : 32 * q + 4, :].bitcast(I32), es_g[4 * q : 4 * q + 4, :].bitcast(I32))
+        nc.vector.tensor_copy(xw_g[:, :P], xw_win[:].bitcast(U32).indirect(offs_t[:, : P // 16]))
         nc.vector.quantize_mx(out=w_codes[:].bitcast(FP8X4), scales=w_scales[:], in_=w_bf[:])
-        for lo, hi in ((0, P), (P, 2 * P), (2 * P, S)):
+        for lo, hi in ((P, 2 * P), (2 * P, S)):
             nc.vector.tensor_copy(xw_g[:, lo:hi], xw_win[:].bitcast(U32).indirect(offs_t[:, lo // 16 : hi // 16]))
         nc.vector.tensor_copy(ew_p[:], ew_win[:].bitcast(U32).indirect(cen_t[:]))
 
         h_ps = [ps.tile([P, PACK, P], F32, name="h_ps%d" % b, tag="bank_a%d" % b) for b in range(BLOCKS)]
-        h_bf = [sb.tile([P, P, PACK], BF16, name="h_bf%d" % b, tag="h_bf%d" % (b % (BLOCKS - 1)), align_bytes=64) for b in range(BLOCKS)]
+        h_bf = [sb.tile([P, P, PACK], BF16, name="h_bf%d" % b, tag="h_bf%d" % b, align_bytes=64) for b in range(BLOCKS)]
         for b in range(BLOCKS):
             for t in range(PACK):
                 nc.tensor.matmul_mx(
@@ -100,16 +101,14 @@ def tile_picked_ystrip_grad_p_kernel(
                     start=True,
                     stop=True,
                 )
-        for b in range(BLOCKS - 1):
+        for b in range(BLOCKS):
             nc.scalar.copy(h_bf[b][:], h_ps[b][:].rearrange("p t n -> p n t"))
 
-        h_codes = sb.tile([P, S], U32, name="h_codes", tag="ew_win", align_bytes=64)
+        h_codes = sb.tile([P, S], U32, name="h_codes", tag="es_g", align_bytes=64)
         h_scales = sb.tile([P, S], U8, name="h_scales", align_bytes=64)
         y_ps = [ps.tile([P, U], F32, name="y_ps%d" % b, tag="bank_y%d" % b) for b in range(BLOCKS)]
         for b in range(BLOCKS):
             cols = slice(b * P, (b + 1) * P)
-            if b == BLOCKS // 2:
-                nc.vector.tensor_copy(h_bf[-1][:], h_ps[-1][:].rearrange("p t n -> p n t"))
             nc.vector.quantize_mx(
                 out=h_codes[:, cols].bitcast(FP8X4),
                 scales=h_scales[:, cols],
@@ -125,15 +124,15 @@ def tile_picked_ystrip_grad_p_kernel(
                 stop=True,
             )
 
-        ex = [sb.tile([P, D, V], F32, name="ex%d" % b, align_bytes=64) for b in range(BLOCKS)]
+        ex = [sb.tile([P, D, V], F32, name="ex%d" % b, tag="ex%d" % b, align_bytes=64) for b in range(BLOCKS)]
         exy = [sb.tile([P, D, V], F32, name="exy%d" % b, align_bytes=64) for b in range(BLOCKS)]
         for b in range(BLOCKS):
             y_dv = y_ps[b][:].rearrange("p (v d) -> p d v", d=D)
             nc.scalar.activation(ex[b][:], y_dv, ACT.Exp, scale=2.0)
             nc.vector.tensor_tensor(exy[b][:], y_dv, ex[b][:], ALU.mult)
 
-        se_ps = ps.tile([P, BLOCKS, P], F32, name="se_ps", tag="bank_a0")
-        ses_ps = ps.tile([P, BLOCKS, P], F32, name="ses_ps", tag="bank_a1")
+        se_ps = ps.tile([P, BLOCKS, P], F32, name="se_ps", tag="bank_a1")
+        ses_half = [ps.tile([P, 2, P], F32, name="ses_ps%d" % i, tag="bank_a%d" % (2 + i)) for i in range(HALVES)]
         addends = {}
         for b in range(BLOCKS):
             for kind, src in (("e", ex), ("y", exy)):
@@ -142,23 +141,24 @@ def tile_picked_ystrip_grad_p_kernel(
                     pair = sb.tile([P, D // 2, V], F32, name="pair%s%d" % (kind, b), align_bytes=64)
                     nc.gpsimd.tensor_tensor(pair[:], src[b][:, : D // 2, :], src[b][:, D // 2 :, :], ALU.add)
                     addends[kind, b] = pair
-        for kind, dst in (("e", se_ps), ("y", ses_ps)):
+        for kind in ("e", "y"):
             for b in range(BLOCKS):
+                dst = se_ps[:, b, :] if kind == "e" else ses_half[b // 2][:, b % 2, :]
                 src = addends[kind, b]
                 count = src.shape[1]
                 for d in range(count):
                     nc.tensor.matmul(
-                        dst[:, b, :], src[:, d, :], ident[:],
+                        dst, src[:, d, :], ident[:],
                         start=(d == 0), stop=(d == count - 1), is_transpose=True,
                     )
 
-        goal_ps = ps.tile([P, BLOCKS, P], F32, name="goal_ps", tag="bank_y0")
+        goal_ps = ps.tile([P, BLOCKS, P], F32, name="goal_ps", tag="bank_a0")
         for b in range(BLOCKS):
             nc.tensor.transpose(goal_ps[:, b, :], goal_t[:, b, :], ident[:])
 
-        margin = sb.tile([P, BLOCKS, P], F32, name="margin", align_bytes=64)
+        margin = sb.tile([P, BLOCKS, P], F32, name="margin", tag="ex3", align_bytes=64)
         nc.vector.tensor_scalar(margin[:], goal_ps[:], -0.9, None, ALU.mult)
-        logit_ps = [ps.tile([P, V], F32, name="logit_ps%d" % b, tag=("bank_a2", "bank_a3", "bank_y1", "bank_y2")[b]) for b in range(BLOCKS)]
+        logit_ps = [ps.tile([P, V], F32, name="logit_ps%d" % b, tag="bank_y%d" % b) for b in range(BLOCKS)]
         for b in range(BLOCKS):
             nc.tensor.matmul(logit_ps[b][:], margin[:, b, :], ident[:], start=True, stop=False, is_transpose=True)
 
@@ -170,7 +170,7 @@ def tile_picked_ystrip_grad_p_kernel(
         for i in range(HALVES):
             nc.scalar.activation(root[:, hs[i], :], se_ps[:, hs[i], :], ACT.Abs_reciprocal_sqrt)
         for i in range(HALVES):
-            nc.vector.scalar_tensor_tensor(mid[:, hs[i], :], ses_ps[:, hs[i], :], 3.0, root[:, hs[i], :], ALU.mult, ALU.mult)
+            nc.vector.scalar_tensor_tensor(mid[:, hs[i], :], ses_half[i][:], 3.0, root[:, hs[i], :], ALU.mult, ALU.mult)
         for i in range(HALVES):
             nc.vector.tensor_tensor(mean3[:, hs[i], :], mid[:, hs[i], :], root[:, hs[i], :], ALU.mult)
         for b in range(BLOCKS):

@@ -137,9 +137,10 @@ def tile_picked_ystrip_grad_p_kernel(
         for b in range(BLOCKS):
             for kind, src in (("e", ex), ("y", exy)):
                 addends[kind, b] = src[b]
-                if kind == "y" and b < BLOCKS // 2:
+                if (kind == "y" and b != BLOCKS - 2) or b == 0:
                     pair = sb.tile([P, D // 2, V], F32, name="pair%s%d" % (kind, b), align_bytes=64)
-                    nc.gpsimd.tensor_tensor(pair[:], src[b][:, : D // 2, :], src[b][:, D // 2 :, :], ALU.add)
+                    adder = nc.vector if b == BLOCKS - 1 else nc.gpsimd
+                    adder.tensor_tensor(pair[:], src[b][:, : D // 2, :], src[b][:, D // 2 :, :], ALU.add)
                     addends[kind, b] = pair
         for kind in ("e", "y"):
             for b in range(BLOCKS):

@@ -36,7 +36,7 @@ def tile_picked_ystrip_grad_p_kernel(
         es_win = sb.tile([P, W], U8, name="es_win", align_bytes=64)
         xw_win = sb.tile([P, T], I32, name="xw_win", align_bytes=64)
         ew_win = sb.tile([P, W], I32, name="ew_win", align_bytes=64)
-        w_raw = [sb.tile([P, PACK, H // HALVES], F32, name="w_raw%d" % i, align_bytes=64) for i in range(HALVES)]
+        w_raw = [sb.tile([P, PACK, H // HALVES], F32, name="w_raw%d" % i, tag="w_raw%d" % i, align_bytes=64) for i in range(HALVES)]
 
 
         nc.gpsimd.memset(xs_win[:].bitcast(I32), 0)
@@ -52,9 +52,6 @@ def tile_picked_ystrip_grad_p_kernel(
         nc.sync.dma_start(es_win[0:16, :].bitcast(I32), e_scales[0].bitcast(I32))
         nc.sync.dma_start(xw_win[:], x_words[0].rearrange("p c r -> p (c r)").bitcast(I32))
         nc.sync.dma_start(ew_win[:], e_words[0].rearrange("p c r -> p (c r)").bitcast(I32))
-
-        goal_t = sb.tile([P, BLOCKS, V], F32, name="goal_t", align_bytes=64)
-        nc.sync.dma_start(goal_t[:], goal.rearrange("(b p) v -> p b v", p=P))
 
         ident = sb.tile([P, P], F32, name="ident")
         make_identity(nc, ident[:])
@@ -82,6 +79,8 @@ def tile_picked_ystrip_grad_p_kernel(
         nc.vector.tensor_copy(es_g[:], es_win[:].indirect(cen_t[:]))
         for q in range(4):
             nc.sync.dma_start(es_p[32 * q : 32 * q + 4, :].bitcast(I32), es_g[4 * q : 4 * q + 4, :].bitcast(I32))
+        goal_t = sb.tile([P, BLOCKS, V], F32, name="goal_t", tag="w_raw1", align_bytes=64)
+        nc.sync.dma_start(goal_t[:], goal.rearrange("(b p) v -> p b v", p=P))
         nc.vector.tensor_copy(xw_g[:, :P], xw_win[:].bitcast(U32).indirect(offs_t[:, : P // 16]))
         nc.vector.quantize_mx(out=w_codes[:].bitcast(FP8X4), scales=w_scales[:], in_=w_bf[:])
         for lo, hi in ((P, 2 * P), (2 * P, S)):
@@ -106,7 +105,8 @@ def tile_picked_ystrip_grad_p_kernel(
 
         h_codes = sb.tile([P, S], U32, name="h_codes", tag="es_g", align_bytes=64)
         h_scales = sb.tile([P, S], U8, name="h_scales", align_bytes=64)
-        y_ps = [ps.tile([P, U], F32, name="y_ps%d" % b, tag="bank_y%d" % b) for b in range(BLOCKS)]
+        y_banks = ("bank_y0", "bank_y1", "bank_y2", "bank_a0")
+        y_ps = [ps.tile([P, U], F32, name="y_ps%d" % b, tag=y_banks[b]) for b in range(BLOCKS)]
         for b in range(BLOCKS):
             cols = slice(b * P, (b + 1) * P)
             nc.vector.quantize_mx(
@@ -153,13 +153,13 @@ def tile_picked_ystrip_grad_p_kernel(
                         start=(d == 0), stop=(d == count - 1), is_transpose=True,
                     )
 
-        goal_ps = ps.tile([P, BLOCKS, P], F32, name="goal_ps", tag="bank_a0")
+        goal_ps = ps.tile([P, BLOCKS, P], F32, name="goal_ps", tag="bank_g")
         for b in range(BLOCKS):
             nc.tensor.transpose(goal_ps[:, b, :], goal_t[:, b, :], ident[:])
 
         margin = sb.tile([P, BLOCKS, P], F32, name="margin", tag="ex3", align_bytes=64)
         nc.vector.tensor_scalar(margin[:], goal_ps[:], -0.9, None, ALU.mult)
-        logit_ps = [ps.tile([P, V], F32, name="logit_ps%d" % b, tag="bank_y%d" % b) for b in range(BLOCKS)]
+        logit_ps = [ps.tile([P, V], F32, name="logit_ps%d" % b, tag=y_banks[b]) for b in range(BLOCKS)]
         for b in range(BLOCKS):
             nc.tensor.matmul(logit_ps[b][:], margin[:, b, :], ident[:], start=True, stop=False, is_transpose=True)
 

@@ -32,24 +32,24 @@ def tile_picked_ystrip_grad_p_kernel(
 
         offs_t = sb.tile([P, S // 16], U16, name="offs_t")
         cen_t = sb.tile([P, U // 16], U16, name="cen_t")
-        xs_win = sb.tile([P, T], U8, name="xs_win", align_bytes=64)
+        xs_win = sb.tile([P, T], U8, name="xs_win", tag="xs_win", align_bytes=64)
         es_win = sb.tile([P, W], U8, name="es_win", align_bytes=64)
         xw_win = sb.tile([P, T], I32, name="xw_win", align_bytes=64)
         ew_win = sb.tile([P, W], I32, name="ew_win", align_bytes=64)
         w_raw = [sb.tile([P, PACK, H // HALVES], F32, name="w_raw%d" % i, tag="w_raw%d" % i, align_bytes=64) for i in range(HALVES)]
 
 
-        nc.gpsimd.memset(xs_win[:].bitcast(I32), 0)
         nc.gpsimd.memset(es_win[:].bitcast(I32), 0)
+        nc.gpsimd.memset(xs_win[:].bitcast(I32), 0)
 
         w_rows = w1.rearrange("(p j) c -> p j c", j=PACK)
-        nc.sync.dma_start(offs_t[:], offs)
         nc.sync.dma_start(cen_t[:], cen)
+        nc.sync.dma_start(offs_t[:], offs)
         nc.sync.dma_start(w_raw[0][:], w_rows[:, :, : H // HALVES])
+        nc.sync.dma_start(es_win[0:16, :].bitcast(I32), e_scales[0].bitcast(I32))
+        nc.sync.dma_start(w_raw[1][:], w_rows[:, :, H // HALVES :])
         for r in range(4):
             nc.sync.dma_start(xs_win[r:P:32, :].bitcast(I32), x_scales[0, r:16:4, :].bitcast(I32))
-        nc.sync.dma_start(w_raw[1][:], w_rows[:, :, H // HALVES :])
-        nc.sync.dma_start(es_win[0:16, :].bitcast(I32), e_scales[0].bitcast(I32))
         nc.sync.dma_start(xw_win[:], x_words[0].rearrange("p c r -> p (c r)").bitcast(I32))
         nc.sync.dma_start(ew_win[:], e_words[0].rearrange("p c r -> p (c r)").bitcast(I32))
 
@@ -72,11 +72,11 @@ def tile_picked_ystrip_grad_p_kernel(
         ew_p = sb.tile([P, U], U32, name="ew_p", align_bytes=64)
         xw_g = sb.tile([P, S], U32, name="xw_g", align_bytes=64)
         w_codes = sb.tile([P, H], U32, name="w_codes", align_bytes=64)
-        w_scales = sb.tile([P, H], U8, name="w_scales", align_bytes=64)
+        w_scales = sb.tile([P, H], U8, name="w_scales", tag="xs_win", align_bytes=64)
 
         nc.gpsimd.memset(es_p[:].bitcast(I32), 0)
-        nc.vector.tensor_copy(xs_all[:], xs_win[:].indirect(offs_t[:]))
         nc.vector.tensor_copy(es_g[:], es_win[:].indirect(cen_t[:]))
+        nc.vector.tensor_copy(xs_all[:], xs_win[:].indirect(offs_t[:]))
         for q in range(4):
             nc.sync.dma_start(es_p[32 * q : 32 * q + 4, :].bitcast(I32), es_g[4 * q : 4 * q + 4, :].bitcast(I32))
         goal_t = sb.tile([P, BLOCKS, V], F32, name="goal_t", tag="w_raw1", align_bytes=64)
@@ -88,7 +88,7 @@ def tile_picked_ystrip_grad_p_kernel(
         nc.vector.tensor_copy(ew_p[:], ew_win[:].bitcast(U32).indirect(cen_t[:]))
 
         h_ps = [ps.tile([P, PACK, P], F32, name="h_ps%d" % b, tag="bank_a%d" % b) for b in range(BLOCKS)]
-        h_bf = [sb.tile([P, P, PACK], BF16, name="h_bf%d" % b, tag="h_bf%d" % b, align_bytes=64) for b in range(BLOCKS)]
+        h_bf = [sb.tile([P, P, PACK], BF16, name="h_bf%d" % b, tag="h_bf%d" % (b % (BLOCKS - 1)), align_bytes=64) for b in range(BLOCKS)]
         for b in range(BLOCKS):
             for t in range(PACK):
                 nc.tensor.matmul_mx(
@@ -100,7 +100,7 @@ def tile_picked_ystrip_grad_p_kernel(
                     start=True,
                     stop=True,
                 )
-        for b in range(BLOCKS):
+        for b in range(BLOCKS - 1):
             nc.scalar.copy(h_bf[b][:], h_ps[b][:].rearrange("p t n -> p n t"))
 
         h_codes = sb.tile([P, S], U32, name="h_codes", tag="es_g", align_bytes=64)
@@ -109,6 +109,8 @@ def tile_picked_ystrip_grad_p_kernel(
         y_ps = [ps.tile([P, U], F32, name="y_ps%d" % b, tag=y_banks[b]) for b in range(BLOCKS)]
         for b in range(BLOCKS):
             cols = slice(b * P, (b + 1) * P)
+            if b == BLOCKS // 2:
+                nc.vector.tensor_copy(h_bf[-1][:], h_ps[-1][:].rearrange("p t n -> p n t"))
             nc.vector.quantize_mx(
                 out=h_codes[:, cols].bitcast(FP8X4),
                 scales=h_scales[:, cols],

@@ -28,6 +28,7 @@ def tile_picked_ystrip_grad_p_kernel(
     nc = tc.nc
     with ExitStack() as ctx:
         sb = ctx.enter_context(tc.tile_pool(name="sb", bufs=1))
+        held = ctx.enter_context(tc.tile_pool(name="held", bufs=1))
         ps = ctx.enter_context(tc.psum_pool(name="ps", bufs=1))
 
         offs_t = sb.tile([P, S // 16], U16, name="offs_t")
@@ -36,21 +37,22 @@ def tile_picked_ystrip_grad_p_kernel(
         es_win = sb.tile([P, W], U8, name="es_win", align_bytes=64)
         xw_win = sb.tile([P, T], I32, name="xw_win", align_bytes=64)
         ew_win = sb.tile([P, W], I32, name="ew_win", align_bytes=64)
-        w_raw = [sb.tile([P, PACK, H // HALVES], F32, name="w_raw%d" % i, tag="w_raw%d" % i, align_bytes=64) for i in range(HALVES)]
+        w_cut = PACK * 96
+        w_raw = [sb.tile([P, PACK, n], F32, name="w_raw%d" % i, tag="w_raw%d" % i, align_bytes=64) for i, n in enumerate((w_cut, H - w_cut))]
 
 
-        nc.gpsimd.memset(es_win[:].bitcast(I32), 0)
         nc.gpsimd.memset(xs_win[:].bitcast(I32), 0)
+        nc.gpsimd.memset(es_win[0:96, :].bitcast(I32), 0)
 
         w_rows = w1.rearrange("(p j) c -> p j c", j=PACK)
         nc.sync.dma_start(cen_t[:], cen)
+        nc.sync.dma_start(es_win[96:128, :].bitcast(I32), e_scales[0].bitcast(I32).unsqueeze(1).broadcast_to([16, 2, W // 4]))
+        nc.sync.dma_start(w_raw[0][:], w_rows[:, :, :w_cut])
         nc.sync.dma_start(offs_t[:], offs)
-        nc.sync.dma_start(w_raw[0][:], w_rows[:, :, : H // HALVES])
-        nc.sync.dma_start(es_win[0:16, :].bitcast(I32), e_scales[0].bitcast(I32))
-        nc.sync.dma_start(w_raw[1][:], w_rows[:, :, H // HALVES :])
         for r in range(4):
             nc.sync.dma_start(xs_win[r:P:32, :].bitcast(I32), x_scales[0, r:16:4, :].bitcast(I32))
         nc.sync.dma_start(xw_win[:], x_words[0].rearrange("p c r -> p (c r)").bitcast(I32))
+        nc.sync.dma_start(w_raw[1][:], w_rows[:, :, w_cut:])
         nc.sync.dma_start(ew_win[:], e_words[0].rearrange("p c r -> p (c r)").bitcast(I32))
 
         ident = sb.tile([P, P], F32, name="ident")
@@ -58,19 +60,20 @@ def tile_picked_ystrip_grad_p_kernel(
 
         w_bf = sb.tile([P, PACK * H], BF16, name="w_bf", tag="w_bf", align_bytes=64)
         w_bf_v = w_bf[:].rearrange("p (t m j) -> p m j t", t=PACK, j=PACK)
-        m_half = P // HALVES
-        for i in range(HALVES):
-            nc.scalar.copy(
-                w_bf_v[:, i * m_half : (i + 1) * m_half],
-                w_raw[i][:].rearrange("p j (m t) -> p m j t", t=PACK),
-            )
+        m_cut = w_cut // PACK
+        nc.scalar.copy(w_bf_v[:, :m_cut], w_raw[0][:].rearrange("p j (m t) -> p m j t", t=PACK))
 
         xs_all = sb.tile([P, S], U8, name="xs_all", align_bytes=64)
         xs_g = [xs_all[:, b * P : (b + 1) * P] for b in range(BLOCKS)]
-        es_g = sb.tile([P, U], U8, name="es_g", tag="es_g", align_bytes=64)
+        es_g = held.tile([P, U], U8, name="es_g", align_bytes=64, offset=4 * S - U // 2)
         es_p = sb.tile([P, U], U8, name="es_p", align_bytes=64)
-        ew_p = sb.tile([P, U], U32, name="ew_p", align_bytes=64)
-        xw_g = sb.tile([P, S], U32, name="xw_g", align_bytes=64)
+        ew_p = [
+            sb.tile([P, U // 2], U32, name="ew_early", align_bytes=64),
+            held.tile([P, U // 2], U32, name="ew_late", align_bytes=64, offset=4 * S),
+        ]
+        xw_early = sb.tile([P, S // 2], U32, name="xw_early", align_bytes=64)
+        xw_late = sb.tile([P, S // 2], U32, name="xw_late", tag="w_raw1", align_bytes=64)
+        xw_g = [half[:, b * P : (b + 1) * P] for half in (xw_early, xw_late) for b in range(2)]
         w_codes = sb.tile([P, H], U32, name="w_codes", align_bytes=64)
         w_scales = sb.tile([P, H], U8, name="w_scales", tag="xs_win", align_bytes=64)
 
@@ -78,14 +81,19 @@ def tile_picked_ystrip_grad_p_kernel(
         nc.vector.tensor_copy(es_g[:], es_win[:].indirect(cen_t[:]))
         nc.vector.tensor_copy(xs_all[:], xs_win[:].indirect(offs_t[:]))
         for q in range(4):
-            nc.sync.dma_start(es_p[32 * q : 32 * q + 4, :].bitcast(I32), es_g[4 * q : 4 * q + 4, :].bitcast(I32))
-        goal_t = sb.tile([P, BLOCKS, V], F32, name="goal_t", tag="w_raw1", align_bytes=64)
+            nc.sync.dma_start(es_p[32 * q : 32 * q + 4, :].bitcast(I32), es_g[96 + 8 * q : 96 + 8 * q + 8 : 2, :].bitcast(I32))
+        goal_t = sb.tile([P, BLOCKS, V], F32, name="goal_t", tag="w_raw0", align_bytes=64)
         nc.sync.dma_start(goal_t[:], goal.rearrange("(b p) v -> p b v", p=P))
-        nc.vector.tensor_copy(xw_g[:, :P], xw_win[:].bitcast(U32).indirect(offs_t[:, : P // 16]))
-        nc.vector.quantize_mx(out=w_codes[:].bitcast(FP8X4), scales=w_scales[:], in_=w_bf[:])
-        for lo, hi in ((P, 2 * P), (2 * P, S)):
-            nc.vector.tensor_copy(xw_g[:, lo:hi], xw_win[:].bitcast(U32).indirect(offs_t[:, lo // 16 : hi // 16]))
-        nc.vector.tensor_copy(ew_p[:], ew_win[:].bitcast(U32).indirect(cen_t[:]))
+        nc.vector.tensor_copy(xw_early[:], xw_win[:].bitcast(U32).indirect(offs_t[:, : S // 32]))
+        nc.vector.tensor_copy(w_bf_v[:, m_cut:], w_raw[1][:].rearrange("p j (m t) -> p m j t", t=PACK))
+        for t in range(PACK):
+            nc.vector.quantize_mx(
+                out=w_codes[:, t * P : (t + 1) * P].bitcast(FP8X4),
+                scales=w_scales[:, t * P : (t + 1) * P],
+                in_=w_bf[:, t * H : (t + 1) * H],
+            )
+        nc.vector.tensor_copy(xw_late[:], xw_win[:].bitcast(U32).indirect(offs_t[:, S // 32 :]))
+        nc.vector.tensor_copy(ew_p[0][:], ew_win[:].bitcast(U32).indirect(cen_t[:, : U // 32]))
 
         h_ps = [ps.tile([P, PACK, P], F32, name="h_ps%d" % b, tag="bank_a%d" % b) for b in range(BLOCKS)]
         h_bf = [sb.tile([P, P, PACK], BF16, name="h_bf%d" % b, tag="h_bf%d" % (b % (BLOCKS - 1)), align_bytes=64) for b in range(BLOCKS)]
@@ -95,7 +103,7 @@ def tile_picked_ystrip_grad_p_kernel(
                     out=h_ps[b][:, t, :],
                     lhsT=w_codes[:, t * P : (t + 1) * P].bitcast(FP8X4),
                     lhsT_scale=w_scales[:, t * P : (t + 1) * P],
-                    rhs=xw_g[:, b * P : (b + 1) * P].bitcast(FP8X4),
+                    rhs=xw_g[b].bitcast(FP8X4),
                     rhs_scale=xs_g[b],
                     start=True,
                     stop=True,
@@ -103,35 +111,42 @@ def tile_picked_ystrip_grad_p_kernel(
         for b in range(BLOCKS - 1):
             nc.scalar.copy(h_bf[b][:], h_ps[b][:].rearrange("p t n -> p n t"))
 
-        h_codes = sb.tile([P, S], U32, name="h_codes", tag="es_g", align_bytes=64)
+        h_codes = held.tile([P, S], U32, name="h_codes", align_bytes=64, offset=0)
         h_scales = sb.tile([P, S], U8, name="h_scales", align_bytes=64)
         y_banks = ("bank_y0", "bank_y1", "bank_y2", "bank_a0")
         y_ps = [ps.tile([P, U], F32, name="y_ps%d" % b, tag=y_banks[b]) for b in range(BLOCKS)]
+        y_late = ps.tile([P, U // 2], F32, name="y_late", tag="bank_a1")
+        y_half = [[y_ps[b][:, : U // 2], y_late[:] if b == 0 else y_ps[b][:, U // 2 :]] for b in range(BLOCKS)]
         for b in range(BLOCKS):
             cols = slice(b * P, (b + 1) * P)
-            if b == BLOCKS // 2:
+            if b == BLOCKS - 1:
                 nc.vector.tensor_copy(h_bf[-1][:], h_ps[-1][:].rearrange("p t n -> p n t"))
             nc.vector.quantize_mx(
                 out=h_codes[:, cols].bitcast(FP8X4),
                 scales=h_scales[:, cols],
                 in_=h_bf[b][:].rearrange("p n t -> p (n t)"),
             )
-            nc.tensor.matmul_mx(
-                out=y_ps[b][:],
-                lhsT=h_codes[:, cols].bitcast(FP8X4),
-                lhsT_scale=h_scales[:, cols],
-                rhs=ew_p[:].bitcast(FP8X4),
-                rhs_scale=es_p[:],
-                start=True,
-                stop=True,
-            )
+            for i in range(HALVES):
+                if b == 0 and i == 1:
+                    nc.vector.tensor_copy(ew_p[1][:], ew_win[:].bitcast(U32).indirect(cen_t[:, U // 32 :]))
+                nc.tensor.matmul_mx(
+                    out=y_half[b][i],
+                    lhsT=h_codes[:, cols].bitcast(FP8X4),
+                    lhsT_scale=h_scales[:, cols],
+                    rhs=ew_p[i][:].bitcast(FP8X4),
+                    rhs_scale=es_p[:, i * U // 2 : (i + 1) * U // 2],
+                    start=True,
+                    stop=True,
+                )
 
         ex = [sb.tile([P, D, V], F32, name="ex%d" % b, tag="ex%d" % b, align_bytes=64) for b in range(BLOCKS)]
         exy = [sb.tile([P, D, V], F32, name="exy%d" % b, align_bytes=64) for b in range(BLOCKS)]
         for b in range(BLOCKS):
-            y_dv = y_ps[b][:].rearrange("p (v d) -> p d v", d=D)
-            nc.scalar.activation(ex[b][:], y_dv, ACT.Exp, scale=2.0)
-            nc.vector.tensor_tensor(exy[b][:], y_dv, ex[b][:], ALU.mult)
+            parts = [(y_half[0][i], slice(i * V // 2, (i + 1) * V // 2)) for i in range(HALVES)] if b == 0 else [(y_ps[b][:], slice(0, V))]
+            for y_part, classes in parts:
+                y_dv = y_part.rearrange("p (v d) -> p d v", d=D)
+                nc.scalar.activation(ex[b][:, :, classes], y_dv, ACT.Exp, scale=2.0)
+                nc.vector.tensor_tensor(exy[b][:, :, classes], y_dv, ex[b][:, :, classes], ALU.mult)
 
         se_ps = ps.tile([P, BLOCKS, P], F32, name="se_ps", tag="bank_a1")
         ses_half = [ps.tile([P, 2, P], F32, name="ses_ps%d" % i, tag="bank_a%d" % (2 + i)) for i in range(HALVES)]

@@ -46,7 +46,7 @@ def tile_picked_ystrip_grad_p_kernel(
 
         w_rows = w1.rearrange("(p j) c -> p j c", j=PACK)
         nc.sync.dma_start(cen_t[:], cen)
-        nc.sync.dma_start(es_win[96:128, :].bitcast(I32), e_scales[0].bitcast(I32).unsqueeze(1).broadcast_to([16, 2, W // 4]))
+        nc.scalar.dma_start(es_win[96:128, :].bitcast(I32), e_scales[0].bitcast(I32).unsqueeze(1).broadcast_to([16, 2, W // 4]))
         nc.sync.dma_start(w_raw[0][:], w_rows[:, :, :w_cut])
         nc.sync.dma_start(offs_t[:], offs)
         for r in range(4):
@@ -71,9 +71,9 @@ def tile_picked_ystrip_grad_p_kernel(
             sb.tile([P, U // 2], U32, name="ew_early", align_bytes=64),
             held.tile([P, U // 2], U32, name="ew_late", align_bytes=64, offset=4 * S),
         ]
-        xw_early = sb.tile([P, S // 2], U32, name="xw_early", align_bytes=64)
-        xw_late = sb.tile([P, S // 2], U32, name="xw_late", tag="w_raw1", align_bytes=64)
-        xw_g = [half[:, b * P : (b + 1) * P] for half in (xw_early, xw_late) for b in range(2)]
+        xw_early = sb.tile([P, P], U32, name="xw_early", align_bytes=64)
+        xw_late = sb.tile([P, S - P], U32, name="xw_late", tag="w_raw1", align_bytes=64)
+        xw_g = [xw_early[:]] + [xw_late[:, b * P : (b + 1) * P] for b in range(BLOCKS - 1)]
         w_codes = sb.tile([P, H], U32, name="w_codes", align_bytes=64)
         w_scales = sb.tile([P, H], U8, name="w_scales", tag="xs_win", align_bytes=64)
 
@@ -84,19 +84,24 @@ def tile_picked_ystrip_grad_p_kernel(
             nc.sync.dma_start(es_p[32 * q : 32 * q + 4, :].bitcast(I32), es_g[96 + 8 * q : 96 + 8 * q + 8 : 2, :].bitcast(I32))
         goal_t = sb.tile([P, BLOCKS, V], F32, name="goal_t", tag="w_raw0", align_bytes=64)
         nc.sync.dma_start(goal_t[:], goal.rearrange("(b p) v -> p b v", p=P))
-        nc.vector.tensor_copy(xw_early[:], xw_win[:].bitcast(U32).indirect(offs_t[:, : S // 32]))
-        nc.vector.tensor_copy(w_bf_v[:, m_cut:], w_raw[1][:].rearrange("p j (m t) -> p m j t", t=PACK))
-        for t in range(PACK):
+        nc.vector.tensor_copy(xw_early[:], xw_win[:].bitcast(U32).indirect(offs_t[:, : P // 16]))
+        w_tail = w_raw[1][:].rearrange("p j (m t) -> p m j t", t=PACK)
+        m_scalar = 12
+        nc.scalar.copy(w_bf_v[:, m_cut : m_cut + m_scalar], w_tail[:, :m_scalar])
+        nc.vector.tensor_copy(w_bf_v[:, m_cut + m_scalar :], w_tail[:, m_scalar:])
+        for i in range(HALVES):
+            cols = slice(i * H // 2, (i + 1) * H // 2)
             nc.vector.quantize_mx(
-                out=w_codes[:, t * P : (t + 1) * P].bitcast(FP8X4),
-                scales=w_scales[:, t * P : (t + 1) * P],
-                in_=w_bf[:, t * H : (t + 1) * H],
+                out=w_codes[:, cols].bitcast(FP8X4),
+                scales=w_scales[:, cols],
+                in_=w_bf[:, i * 2 * H : (i + 1) * 2 * H],
             )
-        nc.vector.tensor_copy(xw_late[:], xw_win[:].bitcast(U32).indirect(offs_t[:, S // 32 :]))
+        for lo, hi in ((P, 2 * P), (2 * P, S)):
+            nc.vector.tensor_copy(xw_late[:, lo - P : hi - P], xw_win[:].bitcast(U32).indirect(offs_t[:, lo // 16 : hi // 16]))
         nc.vector.tensor_copy(ew_p[0][:], ew_win[:].bitcast(U32).indirect(cen_t[:, : U // 32]))
 
         h_ps = [ps.tile([P, PACK, P], F32, name="h_ps%d" % b, tag="bank_a%d" % b) for b in range(BLOCKS)]
-        h_bf = [sb.tile([P, P, PACK], BF16, name="h_bf%d" % b, tag="h_bf%d" % (b % (BLOCKS - 1)), align_bytes=64) for b in range(BLOCKS)]
+        h_bf = [sb.tile([P, P, PACK], BF16, name="h_bf%d" % b, tag="h_bf%d" % b, align_bytes=64) for b in range(BLOCKS)]
         for b in range(BLOCKS):
             for t in range(PACK):
                 nc.tensor.matmul_mx(
@@ -108,7 +113,7 @@ def tile_picked_ystrip_grad_p_kernel(
                     start=True,
                     stop=True,
                 )
-        for b in range(BLOCKS - 1):
+        for b in range(BLOCKS):
             nc.scalar.copy(h_bf[b][:], h_ps[b][:].rearrange("p t n -> p n t"))
 
         h_codes = held.tile([P, S], U32, name="h_codes", align_bytes=64, offset=0)
@@ -119,8 +124,6 @@ def tile_picked_ystrip_grad_p_kernel(
         y_half = [[y_ps[b][:, : U // 2], y_late[:] if b == 0 else y_ps[b][:, U // 2 :]] for b in range(BLOCKS)]
         for b in range(BLOCKS):
             cols = slice(b * P, (b + 1) * P)
-            if b == BLOCKS - 1:
-                nc.vector.tensor_copy(h_bf[-1][:], h_ps[-1][:].rearrange("p t n -> p n t"))
             nc.vector.quantize_mx(
                 out=h_codes[:, cols].bitcast(FP8X4),
                 scales=h_scales[:, cols],
@@ -148,6 +151,10 @@ def tile_picked_ystrip_grad_p_kernel(
                 nc.scalar.activation(ex[b][:, :, classes], y_dv, ACT.Exp, scale=2.0)
                 nc.vector.tensor_tensor(exy[b][:, :, classes], y_dv, ex[b][:, :, classes], ALU.mult)
 
+        goal_ps = ps.tile([P, BLOCKS, P], F32, name="goal_ps", tag="bank_g")
+        for b in range(BLOCKS):
+            nc.tensor.transpose(goal_ps[:, b, :], goal_t[:, b, :], ident[:])
+
         se_ps = ps.tile([P, BLOCKS, P], F32, name="se_ps", tag="bank_a1")
         ses_half = [ps.tile([P, 2, P], F32, name="ses_ps%d" % i, tag="bank_a%d" % (2 + i)) for i in range(HALVES)]
         addends = {}
@@ -169,10 +176,6 @@ def tile_picked_ystrip_grad_p_kernel(
                         dst, src[:, d, :], ident[:],
                         start=(d == 0), stop=(d == count - 1), is_transpose=True,
                     )
-
-        goal_ps = ps.tile([P, BLOCKS, P], F32, name="goal_ps", tag="bank_g")
-        for b in range(BLOCKS):
-            nc.tensor.transpose(goal_ps[:, b, :], goal_t[:, b, :], ident[:])
 
         margin = sb.tile([P, BLOCKS, P], F32, name="margin", tag="ex3", align_bytes=64)
         nc.vector.tensor_scalar(margin[:], goal_ps[:], -0.9, None, ALU.mult)

@@ -100,6 +100,17 @@ def tile_picked_ystrip_grad_p_kernel(
             nc.vector.tensor_copy(xw_late[:, lo - P : hi - P], xw_win[:].bitcast(U32).indirect(offs_t[:, lo // 16 : hi // 16]))
         nc.vector.tensor_copy(ew_p[0][:], ew_win[:].bitcast(U32).indirect(cen_t[:, : U // 32]))
 
+        warm_ps = ps.tile([P, P], F32, name="warm_ps", tag="bank_y0")
+        for i in range(5):
+            nc.tensor.matmul_mx(
+                out=warm_ps[:],
+                lhsT=xw_g[0].bitcast(FP8X4),
+                lhsT_scale=xs_g[0],
+                rhs=xw_g[0].bitcast(FP8X4),
+                rhs_scale=xs_g[0],
+                start=True,
+                stop=True,
+            )
         h_ps = [ps.tile([P, PACK, P], F32, name="h_ps%d" % b, tag="bank_a%d" % b) for b in range(BLOCKS)]
         h_bf = [sb.tile([P, P, PACK], BF16, name="h_bf%d" % b, tag="h_bf%d" % b, align_bytes=64) for b in range(BLOCKS)]
         for b in range(BLOCKS):

@@ -172,9 +172,9 @@ def tile_picked_ystrip_grad_p_kernel(
         for b in range(BLOCKS):
             for kind, src in (("e", ex), ("y", exy)):
                 addends[kind, b] = src[b]
-                if (kind == "y" and b != BLOCKS - 2) or b == 0:
+                if kind == "y" or b == 0:
                     pair = sb.tile([P, D // 2, V], F32, name="pair%s%d" % (kind, b), align_bytes=64)
-                    adder = nc.vector if b == BLOCKS - 1 else nc.gpsimd
+                    adder = nc.vector if b >= BLOCKS // 2 else nc.gpsimd
                     adder.tensor_tensor(pair[:], src[b][:, : D // 2, :], src[b][:, D // 2 :, :], ALU.add)
                     addends[kind, b] = pair
         for kind in ("e", "y"):

@@ -162,11 +162,11 @@ def tile_picked_ystrip_grad_p_kernel(
                 nc.scalar.activation(ex[b][:, :, classes], y_dv, ACT.Exp, scale=2.0)
                 nc.vector.tensor_tensor(exy[b][:, :, classes], y_dv, ex[b][:, :, classes], ALU.mult)
 
-        goal_ps = ps.tile([P, BLOCKS, P], F32, name="goal_ps", tag="bank_g")
+        goal_ps = ps.tile([P, BLOCKS, P], F32, name="goal_ps", tag="bank_a1")
         for b in range(BLOCKS):
             nc.tensor.transpose(goal_ps[:, b, :], goal_t[:, b, :], ident[:])
 
-        se_ps = ps.tile([P, BLOCKS, P], F32, name="se_ps", tag="bank_a1")
+        se_ps = ps.tile([P, BLOCKS, P], F32, name="se_ps", tag="bank_g")
         ses_half = [ps.tile([P, 2, P], F32, name="ses_ps%d" % i, tag="bank_a%d" % (2 + i)) for i in range(HALVES)]
         addends = {}
         for b in range(BLOCKS):

@@ -47,8 +47,8 @@ def tile_picked_ystrip_grad_p_kernel(
         w_rows = w1.rearrange("(p j) c -> p j c", j=PACK)
         nc.sync.dma_start(cen_t[:], cen)
         nc.scalar.dma_start(es_win[96:128, :].bitcast(I32), e_scales[0].bitcast(I32).unsqueeze(1).broadcast_to([16, 2, W // 4]))
-        nc.sync.dma_start(w_raw[0][:], w_rows[:, :, :w_cut])
         nc.sync.dma_start(offs_t[:], offs)
+        nc.sync.dma_start(w_raw[0][:], w_rows[:, :, :w_cut])
         for r in range(4):
             nc.sync.dma_start(xs_win[r:P:32, :].bitcast(I32), x_scales[0, r:16:4, :].bitcast(I32))
         nc.sync.dma_start(xw_win[:], x_words[0].rearrange("p c r -> p (c r)").bitcast(I32))
@@ -83,7 +83,8 @@ def tile_picked_ystrip_grad_p_kernel(
         for q in range(4):
             nc.sync.dma_start(es_p[32 * q : 32 * q + 4, :].bitcast(I32), es_g[96 + 8 * q : 96 + 8 * q + 8 : 2, :].bitcast(I32))
         goal_t = sb.tile([P, BLOCKS, V], F32, name="goal_t", tag="w_raw0", align_bytes=64)
-        nc.sync.dma_start(goal_t[:], goal.rearrange("(b p) v -> p b v", p=P))
+        for b in range(BLOCKS):
+            nc.sync.dma_start(goal_t[:, b, :], goal[b * P : (b + 1) * P, :])
         nc.vector.tensor_copy(xw_early[:], xw_win[:].bitcast(U32).indirect(offs_t[:, : P // 16]))
         w_tail = w_raw[1][:].rearrange("p j (m t) -> p m j t", t=PACK)
         m_scalar = 12
@@ -101,7 +102,7 @@ def tile_picked_ystrip_grad_p_kernel(
         nc.vector.tensor_copy(ew_p[0][:], ew_win[:].bitcast(U32).indirect(cen_t[:, : U // 32]))
 
         warm_ps = ps.tile([P, P], F32, name="warm_ps", tag="bank_y0")
-        for i in range(5):
+        for i in range(4):
             nc.tensor.matmul_mx(
                 out=warm_ps[:],
                 lhsT=xw_g[0].bitcast(FP8X4),

@@ -101,17 +101,6 @@ def tile_picked_ystrip_grad_p_kernel(
             nc.vector.tensor_copy(xw_late[:, lo - P : hi - P], xw_win[:].bitcast(U32).indirect(offs_t[:, lo // 16 : hi // 16]))
         nc.vector.tensor_copy(ew_p[0][:], ew_win[:].bitcast(U32).indirect(cen_t[:, : U // 32]))
 
-        warm_ps = ps.tile([P, P], F32, name="warm_ps", tag="bank_y0")
-        for i in range(4):
-            nc.tensor.matmul_mx(
-                out=warm_ps[:],
-                lhsT=xw_g[0].bitcast(FP8X4),
-                lhsT_scale=xs_g[0],
-                rhs=xw_g[0].bitcast(FP8X4),
-                rhs_scale=xs_g[0],
-                start=True,
-                stop=True,
-            )
         h_ps = [ps.tile([P, PACK, P], F32, name="h_ps%d" % b, tag="bank_a%d" % b) for b in range(BLOCKS)]
         h_bf = [sb.tile([P, P, PACK], BF16, name="h_bf%d" % b, tag="h_bf%d" % b, align_bytes=64) for b in range(BLOCKS)]
         for b in range(BLOCKS):
@@ -130,10 +119,32 @@ def tile_picked_ystrip_grad_p_kernel(
 
         h_codes = held.tile([P, S], U32, name="h_codes", align_bytes=64, offset=0)
         h_scales = sb.tile([P, S], U8, name="h_scales", align_bytes=64)
+        y_late = ps.tile([P, U // 2], F32, name="y_late", tag="bank_a1")
         y_banks = ("bank_y0", "bank_y1", "bank_y2", "bank_a0")
         y_ps = [ps.tile([P, U], F32, name="y_ps%d" % b, tag=y_banks[b]) for b in range(BLOCKS)]
-        y_late = ps.tile([P, U // 2], F32, name="y_late", tag="bank_a1")
         y_half = [[y_ps[b][:, : U // 2], y_late[:] if b == 0 else y_ps[b][:, U // 2 :]] for b in range(BLOCKS)]
+        ex = [sb.tile([P, D, V], F32, name="ex%d" % b, tag="ex%d" % b, align_bytes=64) for b in range(BLOCKS)]
+        exy = [sb.tile([P, D, V], F32, name="exy%d" % b, align_bytes=64) for b in range(BLOCKS)]
+
+        def second_product(b, i):
+            cols = slice(b * P, (b + 1) * P)
+            nc.tensor.matmul_mx(
+                out=y_half[b][i],
+                lhsT=h_codes[:, cols].bitcast(FP8X4),
+                lhsT_scale=h_scales[:, cols],
+                rhs=ew_p[i][:].bitcast(FP8X4),
+                rhs_scale=es_p[:, i * U // 2 : (i + 1) * U // 2],
+                start=True,
+                stop=True,
+            )
+
+        def weights(b):
+            parts = [(y_half[0][i], slice(i * V // 2, (i + 1) * V // 2)) for i in range(HALVES)] if b == 0 else [(y_ps[b][:], slice(0, V))]
+            for y_part, classes in parts:
+                y_dv = y_part.rearrange("p (v d) -> p d v", d=D)
+                nc.scalar.activation(ex[b][:, :, classes], y_dv, ACT.Exp, scale=2.0)
+                nc.vector.tensor_tensor(exy[b][:, :, classes], y_dv, ex[b][:, :, classes], ALU.mult)
+
         for b in range(BLOCKS):
             cols = slice(b * P, (b + 1) * P)
             nc.vector.quantize_mx(
@@ -141,27 +152,27 @@ def tile_picked_ystrip_grad_p_kernel(
                 scales=h_scales[:, cols],
                 in_=h_bf[b][:].rearrange("p n t -> p (n t)"),
             )
-            for i in range(HALVES):
-                if b == 0 and i == 1:
-                    nc.vector.tensor_copy(ew_p[1][:], ew_win[:].bitcast(U32).indirect(cen_t[:, U // 32 :]))
-                nc.tensor.matmul_mx(
-                    out=y_half[b][i],
-                    lhsT=h_codes[:, cols].bitcast(FP8X4),
-                    lhsT_scale=h_scales[:, cols],
-                    rhs=ew_p[i][:].bitcast(FP8X4),
-                    rhs_scale=es_p[:, i * U // 2 : (i + 1) * U // 2],
-                    start=True,
-                    stop=True,
-                )
-
-        ex = [sb.tile([P, D, V], F32, name="ex%d" % b, tag="ex%d" % b, align_bytes=64) for b in range(BLOCKS)]
-        exy = [sb.tile([P, D, V], F32, name="exy%d" % b, align_bytes=64) for b in range(BLOCKS)]
-        for b in range(BLOCKS):
-            parts = [(y_half[0][i], slice(i * V // 2, (i + 1) * V // 2)) for i in range(HALVES)] if b == 0 else [(y_ps[b][:], slice(0, V))]
-            for y_part, classes in parts:
-                y_dv = y_part.rearrange("p (v d) -> p d v", d=D)
-                nc.scalar.activation(ex[b][:, :, classes], y_dv, ACT.Exp, scale=2.0)
-                nc.vector.tensor_tensor(exy[b][:, :, classes], y_dv, ex[b][:, :, classes], ALU.mult)
+            if b < BLOCKS - 1:
+                for i in range(HALVES):
+                    if b == 0 and i == 1:
+                        nc.vector.tensor_copy(ew_p[1][:], ew_win[:].bitcast(U32).indirect(cen_t[:, U // 32 :]))
+                    second_product(b, i)
+        for i in range(HALVES):
+            second_product(BLOCKS - 1, i)
+        weights(0)
+        warm_ps = ps.tile([P, P], F32, name="warm_ps", tag="bank_y0")
+        for i in range(4):
+            nc.tensor.matmul_mx(
+                out=warm_ps[:],
+                lhsT=w_codes[:, :P].bitcast(FP8X4),
+                lhsT_scale=w_scales[:, :P],
+                rhs=w_codes[:, :P].bitcast(FP8X4),
+                rhs_scale=w_scales[:, :P],
+                start=True,
+                stop=True,
+            )
+        for b in range(1, BLOCKS):
+            weights(b)
 
         goal_ps = ps.tile([P, BLOCKS, P], F32, name="goal_ps", tag="bank_a1")
         for b in range(BLOCKS):
@@ -191,7 +202,8 @@ def tile_picked_ystrip_grad_p_kernel(
 
         margin = sb.tile([P, BLOCKS, P], F32, name="margin", tag="ex3", align_bytes=64)
         nc.vector.tensor_scalar(margin[:], goal_ps[:], -0.9, None, ALU.mult)
-        logit_ps = [ps.tile([P, V], F32, name="logit_ps%d" % b, tag=y_banks[b]) for b in range(BLOCKS)]
+        logit_banks = ("bank_y0", "bank_y1", "bank_y2", "bank_a0")
+        logit_ps = [ps.tile([P, V], F32, name="logit_ps%d" % b, tag=logit_banks[b]) for b in range(BLOCKS)]
         for b in range(BLOCKS):
             nc.tensor.matmul(logit_ps[b][:], margin[:, b, :], ident[:], start=True, stop=False, is_transpose=True)
 

@@ -42,11 +42,11 @@ def tile_picked_ystrip_grad_p_kernel(
 
 
         nc.gpsimd.memset(xs_win[:].bitcast(I32), 0)
-        nc.gpsimd.memset(es_win[0:96, :].bitcast(I32), 0)
+        nc.gpsimd.memset(es_win[0:112, :].bitcast(I32), 0)
 
         w_rows = w1.rearrange("(p j) c -> p j c", j=PACK)
         nc.sync.dma_start(cen_t[:], cen)
-        nc.scalar.dma_start(es_win[96:128, :].bitcast(I32), e_scales[0].bitcast(I32).unsqueeze(1).broadcast_to([16, 2, W // 4]))
+        nc.scalar.dma_start(es_win[112:128, :].bitcast(I32), e_scales[0].bitcast(I32))
         nc.sync.dma_start(offs_t[:], offs)
         nc.sync.dma_start(w_raw[0][:], w_rows[:, :, :w_cut])
         for r in range(4):
@@ -81,7 +81,7 @@ def tile_picked_ystrip_grad_p_kernel(
         nc.vector.tensor_copy(es_g[:], es_win[:].indirect(cen_t[:]))
         nc.vector.tensor_copy(xs_all[:], xs_win[:].indirect(offs_t[:]))
         for q in range(4):
-            nc.sync.dma_start(es_p[32 * q : 32 * q + 4, :].bitcast(I32), es_g[96 + 8 * q : 96 + 8 * q + 8 : 2, :].bitcast(I32))
+            nc.sync.dma_start(es_p[32 * q : 32 * q + 4, :].bitcast(I32), es_g[112 + 4 * q : 112 + 4 * q + 4, :].bitcast(I32))
         goal_t = sb.tile([P, BLOCKS, V], F32, name="goal_t", tag="w_raw0", align_bytes=64)
         for b in range(BLOCKS):
             nc.sync.dma_start(goal_t[:, b, :], goal[b * P : (b + 1) * P, :])
@@ -184,7 +184,7 @@ def tile_picked_ystrip_grad_p_kernel(
         for b in range(BLOCKS):
             for kind, src in (("e", ex), ("y", exy)):
                 addends[kind, b] = src[b]
-                if kind == "y" or b == 0:
+                if b == 0 or (kind == "y" and b != 2):
                     pair = sb.tile([P, D // 2, V], F32, name="pair%s%d" % (kind, b), align_bytes=64)
                     adder = nc.vector if b >= BLOCKS // 2 else nc.gpsimd
                     adder.tensor_tensor(pair[:], src[b][:, : D // 2, :], src[b][:, D // 2 :, :], ALU.add)

@@ -36,7 +36,7 @@ def tile_picked_ystrip_grad_p_kernel(
         xs_win = sb.tile([P, T], U8, name="xs_win", tag="xs_win", align_bytes=64)
         es_win = sb.tile([P, W], U8, name="es_win", align_bytes=64)
         xw_win = sb.tile([P, T], I32, name="xw_win", align_bytes=64)
-        ew_win = sb.tile([P, W], I32, name="ew_win", align_bytes=64)
+        ew_win = sb.tile([P, W], I32, name="ew_win", tag="ew_win", align_bytes=64)
         w_cut = PACK * 96
         w_raw = [sb.tile([P, PACK, n], F32, name="w_raw%d" % i, tag="w_raw%d" % i, align_bytes=64) for i, n in enumerate((w_cut, H - w_cut))]
 
@@ -102,7 +102,8 @@ def tile_picked_ystrip_grad_p_kernel(
         nc.vector.tensor_copy(ew_p[0][:], ew_win[:].bitcast(U32).indirect(cen_t[:, : U // 32]))
 
         h_ps = [ps.tile([P, PACK, P], F32, name="h_ps%d" % b, tag="bank_a%d" % b) for b in range(BLOCKS)]
-        h_bf = [sb.tile([P, P, PACK], BF16, name="h_bf%d" % b, tag="h_bf%d" % b, align_bytes=64) for b in range(BLOCKS)]
+        h_bf = [sb.tile([P, P, PACK], BF16, name="h_bf%d" % b, tag="h_bf%d" % b, align_bytes=64) for b in range(BLOCKS - 1)]
+        h_last = [sb.tile([P, P // 2, PACK], BF16, name="h_last%d" % i, tag=slot, align_bytes=64) for i, slot in enumerate(("h_last0", "ew_win"))]
         for b in range(BLOCKS):
             for t in range(PACK):
                 nc.tensor.matmul_mx(
@@ -114,8 +115,10 @@ def tile_picked_ystrip_grad_p_kernel(
                     start=True,
                     stop=True,
                 )
-        for b in range(BLOCKS):
+        for b in range(BLOCKS - 1):
             nc.scalar.copy(h_bf[b][:], h_ps[b][:].rearrange("p t n -> p n t"))
+        h_ps_last = h_ps[-1][:].rearrange("p t n -> p n t")
+        nc.scalar.copy(h_last[0][:], h_ps_last[:, : P // 2])
 
         h_codes = held.tile([P, S], U32, name="h_codes", align_bytes=64, offset=0)
         h_scales = sb.tile([P, S], U8, name="h_scales", align_bytes=64)
@@ -147,11 +150,17 @@ def tile_picked_ystrip_grad_p_kernel(
 
         for b in range(BLOCKS):
             cols = slice(b * P, (b + 1) * P)
-            nc.vector.quantize_mx(
-                out=h_codes[:, cols].bitcast(FP8X4),
-                scales=h_scales[:, cols],
-                in_=h_bf[b][:].rearrange("p n t -> p (n t)"),
-            )
+            if b < BLOCKS - 1:
+                pieces = [(cols, h_bf[b])]
+            else:
+                nc.vector.tensor_copy(h_last[1][:], h_ps_last[:, P // 2 :])
+                pieces = [(slice(b * P + i * P // 2, b * P + (i + 1) * P // 2), h_last[i]) for i in range(HALVES)]
+            for part, src in pieces:
+                nc.vector.quantize_mx(
+                    out=h_codes[:, part].bitcast(FP8X4),
+                    scales=h_scales[:, part],
+                    in_=src[:].rearrange("p n t -> p (n t)"),
+                )
             if b < BLOCKS - 1:
                 for i in range(HALVES):
                     if b == 0 and i == 1:
@@ -164,10 +173,10 @@ def tile_picked_ystrip_grad_p_kernel(
         for i in range(4):
             nc.tensor.matmul_mx(
                 out=warm_ps[:],
-                lhsT=w_codes[:, :P].bitcast(FP8X4),
-                lhsT_scale=w_scales[:, :P],
-                rhs=w_codes[:, :P].bitcast(FP8X4),
-                rhs_scale=w_scales[:, :P],
+                lhsT=h_codes[:, S - P :].bitcast(FP8X4),
+                lhsT_scale=h_scales[:, S - P :],
+                rhs=h_codes[:, S - P :].bitcast(FP8X4),
+                rhs_scale=h_scales[:, S - P :],
                 start=True,
                 stop=True,
             )
@@ -184,10 +193,9 @@ def tile_picked_ystrip_grad_p_kernel(
         for b in range(BLOCKS):
             for kind, src in (("e", ex), ("y", exy)):
                 addends[kind, b] = src[b]
-                if b == 0 or (kind == "y" and b != 2):
+                if b == 0 or (kind == "y" and b < BLOCKS // 2):
                     pair = sb.tile([P, D // 2, V], F32, name="pair%s%d" % (kind, b), align_bytes=64)
-                    adder = nc.vector if b >= BLOCKS // 2 else nc.gpsimd
-                    adder.tensor_tensor(pair[:], src[b][:, : D // 2, :], src[b][:, D // 2 :, :], ALU.add)
+                    nc.gpsimd.tensor_tensor(pair[:], src[b][:, : D // 2, :], src[b][:, D // 2 :, :], ALU.add)
                     addends[kind, b] = pair
         for kind in ("e", "y"):
             for b in range(BLOCKS):

@@ -187,13 +187,13 @@ def tile_picked_ystrip_grad_p_kernel(
         for b in range(BLOCKS):
             nc.tensor.transpose(goal_ps[:, b, :], goal_t[:, b, :], ident[:])
 
-        se_ps = ps.tile([P, BLOCKS, P], F32, name="se_ps", tag="bank_g")
+        se_ps = ps.tile([P, BLOCKS, P], F32, name="se_ps", tag="bank_y0")
         ses_half = [ps.tile([P, 2, P], F32, name="ses_ps%d" % i, tag="bank_a%d" % (2 + i)) for i in range(HALVES)]
         addends = {}
         for b in range(BLOCKS):
             for kind, src in (("e", ex), ("y", exy)):
                 addends[kind, b] = src[b]
-                if b == 0 or (kind == "y" and b < BLOCKS // 2):
+                if kind == "y" and b < BLOCKS // 2:
                     pair = sb.tile([P, D // 2, V], F32, name="pair%s%d" % (kind, b), align_bytes=64)
                     nc.gpsimd.tensor_tensor(pair[:], src[b][:, : D // 2, :], src[b][:, D // 2 :, :], ALU.add)
                     addends[kind, b] = pair
@@ -210,7 +210,7 @@ def tile_picked_ystrip_grad_p_kernel(
 
         margin = sb.tile([P, BLOCKS, P], F32, name="margin", tag="ex3", align_bytes=64)
         nc.vector.tensor_scalar(margin[:], goal_ps[:], -0.9, None, ALU.mult)
-        logit_banks = ("bank_y0", "bank_y1", "bank_y2", "bank_a0")
+        logit_banks = ("bank_g", "bank_y1", "bank_y2", "bank_a0")
         logit_ps = [ps.tile([P, V], F32, name="logit_ps%d" % b, tag=logit_banks[b]) for b in range(BLOCKS)]
         for b in range(BLOCKS):
             nc.tensor.matmul(logit_ps[b][:], margin[:, b, :], ident[:], start=True, stop=False, is_transpose=True)

@@ -190,15 +190,9 @@ def tile_picked_ystrip_grad_p_kernel(
         se_ps = ps.tile([P, BLOCKS, P], F32, name="se_ps", tag="bank_y0")
         ses_half = [ps.tile([P, 2, P], F32, name="ses_ps%d" % i, tag="bank_a%d" % (2 + i)) for i in range(HALVES)]
         addends = {}
-        for b in range(BLOCKS):
-            for kind, src in (("e", ex), ("y", exy)):
-                addends[kind, b] = src[b]
-                if kind == "y" and b < BLOCKS // 2:
-                    pair = sb.tile([P, D // 2, V], F32, name="pair%s%d" % (kind, b), align_bytes=64)
-                    nc.gpsimd.tensor_tensor(pair[:], src[b][:, : D // 2, :], src[b][:, D // 2 :, :], ALU.add)
-                    addends[kind, b] = pair
-        for kind in ("e", "y"):
-            for b in range(BLOCKS):
+
+        def add_up(kind, order):
+            for b in order:
                 dst = se_ps[:, b, :] if kind == "e" else ses_half[b // 2][:, b % 2, :]
                 src = addends[kind, b]
                 count = src.shape[1]
@@ -207,6 +201,20 @@ def tile_picked_ystrip_grad_p_kernel(
                         dst, src[:, d, :], ident[:],
                         start=(d == 0), stop=(d == count - 1), is_transpose=True,
                     )
+
+        def pre_add(kind, src, b, adder, slot):
+            pair = sb.tile([P, D // 2, V], F32, name="pair%s%d" % (kind, b), tag=slot, align_bytes=64)
+            adder.tensor_tensor(pair[:], src[b][:, : D // 2, :], src[b][:, D // 2 :, :], ALU.add)
+            addends[kind, b] = pair
+
+        for b in range(BLOCKS):
+            addends["e", b] = ex[b]
+        pre_add("y", exy, 0, nc.gpsimd, "pair_y0")
+        pre_add("y", exy, 1, nc.gpsimd, "pair_y1")
+        add_up("e", range(BLOCKS))
+        pre_add("y", exy, 2, nc.vector, "ex2")
+        addends["y", 3] = exy[3]
+        add_up("y", (0, 1, 3, 2))
 
         margin = sb.tile([P, BLOCKS, P], F32, name="margin", tag="ex3", align_bytes=64)
         nc.vector.tensor_scalar(margin[:], goal_ps[:], -0.9, None, ALU.mult)

@@ -169,17 +169,6 @@ def tile_picked_ystrip_grad_p_kernel(
         for i in range(HALVES):
             second_product(BLOCKS - 1, i)
         weights(0)
-        warm_ps = ps.tile([P, P], F32, name="warm_ps", tag="bank_y0")
-        for i in range(4):
-            nc.tensor.matmul_mx(
-                out=warm_ps[:],
-                lhsT=h_codes[:, S - P :].bitcast(FP8X4),
-                lhsT_scale=h_scales[:, S - P :],
-                rhs=h_codes[:, S - P :].bitcast(FP8X4),
-                rhs_scale=h_scales[:, S - P :],
-                start=True,
-                stop=True,
-            )
         for b in range(1, BLOCKS):
             weights(b)
 

from contextlib import ExitStack

import concourse.mybir as mybir
from concourse.masks import make_identity

K, T, S, H, D, V, W, U = 512, 1024, 512, 512, 4, 128, 2048, 512
FLOPS = 2 * K * H * S + 2 * H * S * U

F32 = mybir.dt.float32
BF16 = mybir.dt.bfloat16
I32 = mybir.dt.int32
U32 = mybir.dt.uint32
U16 = mybir.dt.uint16
U8 = mybir.dt.uint8
FP8X4 = mybir.dt.float8_e4m3fn_x4
ACT = mybir.ActivationFunctionType
ALU = mybir.AluOpType

P = 128
PACK = 4
BLOCKS = S // P
HALVES = 2


def tile_picked_ystrip_grad_p_kernel(
    tc, x_words, x_scales, w1, e_words, e_scales, goal, offs, cen, out
):
    nc = tc.nc
    with ExitStack() as ctx:
        sb = ctx.enter_context(tc.tile_pool(name="sb", bufs=1))
        held = ctx.enter_context(tc.tile_pool(name="held", bufs=1))
        ps = ctx.enter_context(tc.psum_pool(name="ps", bufs=1))

        offs_t = sb.tile([P, S // 16], U16, name="offs_t")
        cen_t = sb.tile([P, U // 16], U16, name="cen_t")
        xs_win = sb.tile([P, T], U8, name="xs_win", tag="xs_win", align_bytes=64)
        es_win = sb.tile([P, W], U8, name="es_win", align_bytes=64)
        xw_win = sb.tile([P, T], I32, name="xw_win", align_bytes=64)
        ew_win = sb.tile([P, W], I32, name="ew_win", tag="ew_win", align_bytes=64)
        w_cut = PACK * 96
        w_raw = [sb.tile([P, PACK, n], F32, name="w_raw%d" % i, tag="w_raw%d" % i, align_bytes=64) for i, n in enumerate((w_cut, H - w_cut))]


        nc.gpsimd.memset(xs_win[:].bitcast(I32), 0)
        nc.gpsimd.memset(es_win[0:112, :].bitcast(I32), 0)

        w_rows = w1.rearrange("(p j) c -> p j c", j=PACK)
        nc.sync.dma_start(cen_t[:], cen)
        nc.scalar.dma_start(es_win[112:128, :].bitcast(I32), e_scales[0].bitcast(I32))
        nc.sync.dma_start(offs_t[:], offs)
        nc.sync.dma_start(w_raw[0][:], w_rows[:, :, :w_cut])
        for r in range(4):
            nc.sync.dma_start(xs_win[r:P:32, :].bitcast(I32), x_scales[0, r:16:4, :].bitcast(I32))
        nc.sync.dma_start(xw_win[:], x_words[0].rearrange("p c r -> p (c r)").bitcast(I32))
        nc.sync.dma_start(w_raw[1][:], w_rows[:, :, w_cut:])
        nc.sync.dma_start(ew_win[:], e_words[0].rearrange("p c r -> p (c r)").bitcast(I32))

        ident = sb.tile([P, P], F32, name="ident")
        make_identity(nc, ident[:])

        w_bf = sb.tile([P, PACK * H], BF16, name="w_bf", tag="w_bf", align_bytes=64)
        w_bf_v = w_bf[:].rearrange("p (t m j) -> p m j t", t=PACK, j=PACK)
        m_cut = w_cut // PACK
        nc.scalar.copy(w_bf_v[:, :m_cut], w_raw[0][:].rearrange("p j (m t) -> p m j t", t=PACK))

        xs_all = sb.tile([P, S], U8, name="xs_all", align_bytes=64)
        xs_g = [xs_all[:, b * P : (b + 1) * P] for b in range(BLOCKS)]
        es_g = held.tile([P, U], U8, name="es_g", align_bytes=64, offset=4 * S - U // 2)
        es_p = sb.tile([P, U], U8, name="es_p", align_bytes=64)
        ew_p = [
            sb.tile([P, U // 2], U32, name="ew_early", align_bytes=64),
            held.tile([P, U // 2], U32, name="ew_late", align_bytes=64, offset=4 * S),
        ]
        xw_early = sb.tile([P, P], U32, name="xw_early", align_bytes=64)
        xw_late = sb.tile([P, S - P], U32, name="xw_late", tag="w_raw1", align_bytes=64)
        xw_g = [xw_early[:]] + [xw_late[:, b * P : (b + 1) * P] for b in range(BLOCKS - 1)]
        w_codes = sb.tile([P, H], U32, name="w_codes", align_bytes=64)
        w_scales = sb.tile([P, H], U8, name="w_scales", tag="xs_win", align_bytes=64)

        nc.gpsimd.memset(es_p[:].bitcast(I32), 0)
        nc.vector.tensor_copy(es_g[:], es_win[:].indirect(cen_t[:]))
        nc.vector.tensor_copy(xs_all[:], xs_win[:].indirect(offs_t[:]))
        for q in range(4):
            nc.sync.dma_start(es_p[32 * q : 32 * q + 4, :].bitcast(I32), es_g[112 + 4 * q : 112 + 4 * q + 4, :].bitcast(I32))
        goal_t = sb.tile([P, BLOCKS, V], F32, name="goal_t", tag="w_raw0", align_bytes=64)
        for b in range(BLOCKS):
            nc.sync.dma_start(goal_t[:, b, :], goal[b * P : (b + 1) * P, :])
        nc.vector.tensor_copy(xw_early[:], xw_win[:].bitcast(U32).indirect(offs_t[:, : P // 16]))
        w_tail = w_raw[1][:].rearrange("p j (m t) -> p m j t", t=PACK)
        m_scalar = 12
        nc.scalar.copy(w_bf_v[:, m_cut : m_cut + m_scalar], w_tail[:, :m_scalar])
        nc.vector.tensor_copy(w_bf_v[:, m_cut + m_scalar :], w_tail[:, m_scalar:])
        for i in range(HALVES):
            cols = slice(i * H // 2, (i + 1) * H // 2)
            nc.vector.quantize_mx(
                out=w_codes[:, cols].bitcast(FP8X4),
                scales=w_scales[:, cols],
                in_=w_bf[:, i * 2 * H : (i + 1) * 2 * H],
            )
        for lo, hi in ((P, 2 * P), (2 * P, S)):
            nc.vector.tensor_copy(xw_late[:, lo - P : hi - P], xw_win[:].bitcast(U32).indirect(offs_t[:, lo // 16 : hi // 16]))
        nc.vector.tensor_copy(ew_p[0][:], ew_win[:].bitcast(U32).indirect(cen_t[:, : U // 32]))

        h_ps = [ps.tile([P, PACK, P], F32, name="h_ps%d" % b, tag="bank_a%d" % b) for b in range(BLOCKS)]
        h_bf = [sb.tile([P, P, PACK], BF16, name="h_bf%d" % b, tag="h_bf%d" % b, align_bytes=64) for b in range(BLOCKS - 1)]
        h_last = [sb.tile([P, P // 2, PACK], BF16, name="h_last%d" % i, tag=slot, align_bytes=64) for i, slot in enumerate(("h_last0", "ew_win"))]
        for b in range(BLOCKS):
            for t in range(PACK):
                nc.tensor.matmul_mx(
                    out=h_ps[b][:, t, :],
                    lhsT=w_codes[:, t * P : (t + 1) * P].bitcast(FP8X4),
                    lhsT_scale=w_scales[:, t * P : (t + 1) * P],
                    rhs=xw_g[b].bitcast(FP8X4),
                    rhs_scale=xs_g[b],
                    start=True,
                    stop=True,
                )
        for b in range(BLOCKS - 1):
            nc.scalar.copy(h_bf[b][:], h_ps[b][:].rearrange("p t n -> p n t"))
        h_ps_last = h_ps[-1][:].rearrange("p t n -> p n t")
        nc.scalar.copy(h_last[0][:], h_ps_last[:, : P // 2])

        h_codes = held.tile([P, S], U32, name="h_codes", align_bytes=64, offset=0)
        h_scales = sb.tile([P, S], U8, name="h_scales", align_bytes=64)
        y_late = ps.tile([P, U // 2], F32, name="y_late", tag="bank_a1")
        y_banks = ("bank_y0", "bank_y1", "bank_y2", "bank_a0")
        y_ps = [ps.tile([P, U], F32, name="y_ps%d" % b, tag=y_banks[b]) for b in range(BLOCKS)]
        y_half = [[y_ps[b][:, : U // 2], y_late[:] if b == 0 else y_ps[b][:, U // 2 :]] for b in range(BLOCKS)]
        ex = [sb.tile([P, D, V], F32, name="ex%d" % b, tag="ex%d" % b, align_bytes=64) for b in range(BLOCKS)]
        exy = [sb.tile([P, D, V], F32, name="exy%d" % b, align_bytes=64) for b in range(BLOCKS)]

        def second_product(b, i):
            cols = slice(b * P, (b + 1) * P)
            nc.tensor.matmul_mx(
                out=y_half[b][i],
                lhsT=h_codes[:, cols].bitcast(FP8X4),
                lhsT_scale=h_scales[:, cols],
                rhs=ew_p[i][:].bitcast(FP8X4),
                rhs_scale=es_p[:, i * U // 2 : (i + 1) * U // 2],
                start=True,
                stop=True,
            )

        def weights(b):
            parts = [(y_half[0][i], slice(i * V // 2, (i + 1) * V // 2)) for i in range(HALVES)] if b == 0 else [(y_ps[b][:], slice(0, V))]
            for y_part, classes in parts:
                y_dv = y_part.rearrange("p (v d) -> p d v", d=D)
                nc.scalar.activation(ex[b][:, :, classes], y_dv, ACT.Exp, scale=2.0)
                nc.vector.tensor_tensor(exy[b][:, :, classes], y_dv, ex[b][:, :, classes], ALU.mult)

        for b in range(BLOCKS):
            cols = slice(b * P, (b + 1) * P)
            if b < BLOCKS - 1:
                pieces = [(cols, h_bf[b])]
            else:
                nc.vector.tensor_copy(h_last[1][:], h_ps_last[:, P // 2 :])
                pieces = [(slice(b * P + i * P // 2, b * P + (i + 1) * P // 2), h_last[i]) for i in range(HALVES)]
            for part, src in pieces:
                nc.vector.quantize_mx(
                    out=h_codes[:, part].bitcast(FP8X4),
                    scales=h_scales[:, part],
                    in_=src[:].rearrange("p n t -> p (n t)"),
                )
            if b < BLOCKS - 1:
                for i in range(HALVES):
                    if b == 0 and i == 1:
                        nc.vector.tensor_copy(ew_p[1][:], ew_win[:].bitcast(U32).indirect(cen_t[:, U // 32 :]))
                    second_product(b, i)
        for i in range(HALVES):
            second_product(BLOCKS - 1, i)
        weights(0)
        for b in range(1, BLOCKS):
            weights(b)

        goal_ps = ps.tile([P, BLOCKS, P], F32, name="goal_ps", tag="bank_a1")
        for b in range(BLOCKS):
            nc.tensor.transpose(goal_ps[:, b, :], goal_t[:, b, :], ident[:])

        se_ps = ps.tile([P, BLOCKS, P], F32, name="se_ps", tag="bank_y0")
        ses_half = [ps.tile([P, 2, P], F32, name="ses_ps%d" % i, tag="bank_a%d" % (2 + i)) for i in range(HALVES)]
        addends = {}

        def add_up(kind, order):
            for b in order:
                dst = se_ps[:, b, :] if kind == "e" else ses_half[b // 2][:, b % 2, :]
                src = addends[kind, b]
                count = src.shape[1]
                for d in range(count):
                    nc.tensor.matmul(
                        dst, src[:, d, :], ident[:],
                        start=(d == 0), stop=(d == count - 1), is_transpose=True,
                    )

        def pre_add(kind, src, b, adder, slot):
            pair = sb.tile([P, D // 2, V], F32, name="pair%s%d" % (kind, b), tag=slot, align_bytes=64)
            adder.tensor_tensor(pair[:], src[b][:, : D // 2, :], src[b][:, D // 2 :, :], ALU.add)
            addends[kind, b] = pair

        for b in range(BLOCKS):
            addends["e", b] = ex[b]
        pre_add("y", exy, 0, nc.gpsimd, "pair_y0")
        pre_add("y", exy, 1, nc.gpsimd, "pair_y1")
        add_up("e", range(BLOCKS))
        pre_add("y", exy, 2, nc.vector, "ex2")
        addends["y", 3] = exy[3]
        add_up("y", (0, 1, 3, 2))

        margin = sb.tile([P, BLOCKS, P], F32, name="margin", tag="ex3", align_bytes=64)
        nc.vector.tensor_scalar(margin[:], goal_ps[:], -0.9, None, ALU.mult)
        logit_banks = ("bank_g", "bank_y1", "bank_y2", "bank_a0")
        logit_ps = [ps.tile([P, V], F32, name="logit_ps%d" % b, tag=logit_banks[b]) for b in range(BLOCKS)]
        for b in range(BLOCKS):
            nc.tensor.matmul(logit_ps[b][:], margin[:, b, :], ident[:], start=True, stop=False, is_transpose=True)

        root = sb.tile([P, BLOCKS, P], F32, name="root", align_bytes=64)
        mid = sb.tile([P, BLOCKS, P], F32, name="mid", align_bytes=64)
        mean3 = sb.tile([P, BLOCKS, P], F32, name="mean3", align_bytes=64)
        negmax = [sb.tile([P, 1], F32, name="negmax%d" % b) for b in range(BLOCKS)]
        hs = [slice(2 * i, 2 * i + 2) for i in range(HALVES)]
        for i in range(HALVES):
            nc.scalar.activation(root[:, hs[i], :], se_ps[:, hs[i], :], ACT.Abs_reciprocal_sqrt)
        for i in range(HALVES):
            nc.vector.scalar_tensor_tensor(mid[:, hs[i], :], ses_half[i][:], 3.0, root[:, hs[i], :], ALU.mult, ALU.mult)
        for i in range(HALVES):
            nc.vector.tensor_tensor(mean3[:, hs[i], :], mid[:, hs[i], :], root[:, hs[i], :], ALU.mult)
        for b in range(BLOCKS):
            nc.tensor.matmul(logit_ps[b][:], mean3[:, b, :], ident[:], start=False, stop=True, is_transpose=True)
            nc.vector.tensor_reduce(negmax[b][:], logit_ps[b][:], mybir.AxisListType.X, ALU.max, negate=True)

        for b in range(BLOCKS):
            prob = sb.tile([P, V], F32, name="prob%d" % b, align_bytes=64)
            total = sb.tile([P, 1], F32, name="total%d" % b)
            inv = sb.tile([P, 1], F32, name="inv%d" % b)
            res = sb.tile([P, V], F32, name="res%d" % b, align_bytes=64)
            nc.scalar.activation(prob[:], logit_ps[b][:], ACT.Exp, bias=negmax[b][:], accum_out=total[:])
            nc.vector.reciprocal(inv[:], total[:])
            nc.vector.scalar_tensor_tensor(res[:], prob[:], inv[:], goal_t[:, b, :], ALU.mult, ALU.subtract)
            nc.sync.dma_start(out[b * P : (b + 1) * P, :], res[:])
